import numpy as np, ml_dtypes
CORES = [78,86,94,102,110,118]
N = 6
import mx_ref
BF = ml_dtypes.bfloat16
def f(rng, *shape):
    return mx_ref.flush((rng.standard_normal(shape, dtype=np.float32) * np.exp2(rng.integers(-2, 3, shape[:-1] + (1,)))).astype(BF))
def wide(rng, *shape, cols=0):
    v = rng.standard_normal(shape, dtype=np.float32) * np.exp2(rng.integers(-12, 13, shape)).astype(np.float32)
    if cols: v *= np.repeat(np.exp2(rng.integers(-cols, cols + 1, shape[:-2] + (1, shape[-1] // 4))) * (rng.random(shape[:-2] + (1, shape[-1] // 4)) > 0.0625), 4, axis=-1).astype(np.float32)
    return mx_ref.flush(v.astype(BF))
T, CAPP, O = 256, 64, 3
def scores(us, x):
    return mx_ref.matmul(mx_ref.quantize(us), mx_ref.quantize(x))[:8] + np.float32(0.0)
def winners(us, x):
    return np.argmax(np.stack([scores(us[s], x[s]) for s in range(N)]), axis=0)
def fill(rng, n, tot, most):
    n = np.array(n)
    while n.sum() < tot:
        q = rng.integers(0, N)
        if n[q] < most[q]: n[q] += 1
    return rng.permutation(np.repeat(np.arange(N), n))
def deal(rng, full):
    return np.stack([fill(rng, [CAPP if q in full[g] else 0 for q in range(N)], T, [CAPP] * N) for g in range(8)])
def one(rng):
    g, s = rng.integers(0, 8), rng.integers(0, N)
    return deal(rng, [[s] if i == g else [] for i in range(8)])
def heads(rng):
    u, h = np.zeros((8, 16, 128, 4), np.float32), np.arange(8)
    u[h, :, h] = rng.choice([-1.0, 1.0], (8, 16, 4)) * (0.25 + np.abs(rng.standard_normal((8, 16, 4)))) * np.exp2(rng.integers(-2, 3, (8, 16, 1)))
    return np.repeat(u.reshape(1, 128, 512).astype(BF), N, axis=0)
def plant(rng, x, us, wn, big=4, tie=None, zero=None):
    v = np.abs(x.astype(np.float32)).reshape(N, 8, 16, T, 4)
    v[v < 2.0 ** -24] = 0
    h, b = np.arange(8), np.float32(big)
    a = np.sign(us.astype(np.float32)).reshape(8, 16, 128, 4)[h, :, h][:, :, None]
    win = (wn == np.arange(N)[:, None, None])[:, :, None, :, None]
    neg = (rng.random((8, T)) < 0.125)[:, None, :, None]
    c = np.where(rng.random(v.shape, dtype=np.float32) < 0.5, np.float32(-1), np.float32(1))
    t = (np.where(neg, np.where(win, -a, -4 * b * a), np.where(win, b * a, c)) * v).astype(np.float32)
    s = np.stack([scores(us, t[r].reshape(128, 4 * T).astype(BF)) for r in range(N)])
    won = np.take_along_axis(s, wn[None], axis=0)[0]
    lost = np.where(win[:, :, 0, :, 0], -np.inf, s).max(axis=0)
    bad = (~(won - lost > 0.5 * np.abs(won)))[:, None, :, None]
    t = np.where(bad, np.where(win, b * a, -a) * v, t).astype(np.float32)
    if tie is not None:
        best = np.where(win, t, np.float32(0)).sum(axis=0)
        t = np.where(tie[:, None, :, None] & (wn < np.arange(N)[:, None, None])[:, :, None, :, None], best, t)
    if zero is not None: t[:, :, :, zero] = 0
    return t.reshape(N, 128, 4 * T).astype(BF)
def narrow(rng, x, us, wn):
    v, h = x.astype(np.float32).reshape(N, 8, 16, T, 4), np.arange(8)
    u = np.abs(us.astype(np.float32)).reshape(8, 16, 128, 4)[h, :, h]
    i, b = np.unravel_index(u.reshape(8, 64).argmin(axis=1), (16, 4))
    win = wn == np.arange(N)[:, None, None]
    part = np.where(win[:, :, None, :, None], v, np.float32(0)).sum(axis=0)
    p = np.exp2(np.floor(np.log2((u[:, :, None] * np.abs(part)).sum(axis=(1, 3))) - np.log2(u[h, i, b])[:, None]) - 12)
    z = np.stack([np.where(part[g, i[g], :, b[g]] < 0, -p[g], p[g]) for g in range(8)])
    close = np.repeat((rng.permutation(T) < T // 3)[None], 8, axis=0)
    other = (wn + rng.integers(1, N, (8, T))) % N
    hold = ((rng.random((N, 8, T)) < 0.25) | (other == np.arange(N)[:, None, None])) & ~win & close
    held = hold | (win & close)
    t = np.where(held[:, :, None, :, None], part, v).astype(np.float32)
    d = np.where(hold, rng.choice([-0.125, 0.125], (N, 8, T)), 0.0)
    for k in range(2):
        for g in range(8): t[:, g, i[g], :, b[g]] = np.where(held[:, g], z[g] * (1.5 + d[:, g]), t[:, g, i[g], :, b[g]])
        s = np.stack([scores(us, t[r].reshape(128, 4 * T).astype(BF)) for r in range(N)])
        if k == 0: d = np.where(s == np.take_along_axis(s, wn[None], axis=0), 2 * d, d)
    now = np.argmax(s, axis=0)
    for g in range(8):
        for k in range(T):
            n = np.bincount(now[g], minlength=N)
            q = n.argmax()
            if n[q] <= CAPP: break
            j = rng.permutation(np.flatnonzero((now[g] == q) & (wn[g] != q)))[:n[q] - CAPP]
            now[g, j] = wn[g, j]; close[g, j] = False
    return np.where(close[:, None, :, None], t, v).reshape(N, 128, 4 * T).astype(BF)
def draw(rng, wn, **k):
    us = heads(rng)
    return {"x": plant(rng, f(rng, N, 128, 4 * T), us[0], wn, **k), "us": us, "w": f(rng, N, 128, 512 * O)}
def setup_inputs(rng):
    return draw(rng, one(rng))
def setup_inputs_equal(rng):
    e, p = CAPP - 8, rng.permutation(T)
    far = np.stack([fill(rng, [8] + [0] * (N - 1), T - e, [8] + [CAPP] * (N - 1)) for g in range(8)])
    wn = np.concatenate([np.zeros((8, e), int), far], axis=1)[:, p]
    tie = np.repeat(np.concatenate([np.ones(e, bool), np.arange(T - e) % 2 == 0])[None], 8, axis=0)[:, p]
    return draw(rng, wn, tie=tie, zero=(np.arange(T) < 4)[p])
def setup_inputs_full(rng):
    s, k = int(rng.integers(0, N)), T // CAPP
    return draw(rng, deal(rng, [[s] + [q for q in rng.permutation(N).tolist() if q != s][:k - 1] for g in range(8)]))
def setup_inputs_near(rng):
    wn = one(rng)
    d = draw(rng, wn); d["x"] = narrow(rng, d["x"], d["us"][0], wn); return d
def setup_inputs_spread(rng):
    wn, us = one(rng), heads(rng)
    e = np.exp2(rng.integers(-4, 5, (N, 8, 1, T, 1))) * ((rng.random((N, 8, 1, T, 1)) > 0.0625) | (wn == np.arange(N)[:, None, None])[:, :, None, :, None])
    x = wide(rng, N, 128, 4 * T).astype(np.float32).reshape(N, 8, 16, T, 4) * e.astype(np.float32)
    return {"x": plant(rng, x, us[0], wn, big=256), "us": us, "w": f(rng, N, 128, 512 * O)}
def setup_inputs_stretch(rng):
    L = []
    for g in range(8):
        s, a = rng.integers(0, N), rng.choice([0, T - CAPP, rng.integers(0, T - CAPP + 1)])
        far = fill(rng, [0] * N, T - CAPP, [0 if q == s else CAPP for q in range(N)])
        L.append(np.concatenate([far[:a], np.full(CAPP, s), far[a:]]))
    return draw(rng, np.stack(L))
def check_inputs(d):
    b = []
    for k in ("x", "us", "w"):
        v = np.abs(np.asarray(d[k]).astype(np.float32))
        if not ((v == 0) | ((v >= 2.0 ** -30) & (v <= 2.0 ** 30))).all(): b.append(k)
    if b: return b
    u, h = np.array(d["us"]).astype(np.float32), np.arange(8)
    same = (u == u[:1]).all()
    u = u.reshape(N, 8, 16, 128, 4); u[:, h, :, h] = 0
    if not same or (u != 0).any(): b.append("us")
    wn = winners(d["us"], d["x"])
    if max((wn == s).sum(axis=1).max() for s in range(N)) > CAPP: b.append("x")
    return b
def reference(x, us, w):
    wn = winners(us, x)
    M = []
    for s in range(N):
        v = np.where((wn == s)[:, None, :, None], x[s].astype(np.float32).reshape(8, 16, T, 4), np.float32(0))
        M.append(mx_ref.quantize(np.ascontiguousarray(v.reshape(128, 4 * T).astype(BF))))
    y = np.zeros((N, 128, O * T), np.float32)
    for r in range(N):
        for o in range(O):
            W = mx_ref.quantize(np.ascontiguousarray(w[r][:, 512 * o:512 * o + 512]))
            for s in range(N): y[r][:, T * o:T * o + T] += mx_ref.matmul(W, M[s])
    return {"y": y, "wn": np.repeat(wn.astype(np.float32)[None], N, axis=0)}

@@ -1,0 +1,447 @@
+from concourse.bass import DstId, RemoteDMATransfer
+from concourse.mybir import dt, AluOpType, ActivationFunctionType
+
+NP = 8
+PW = 384
+CAP = 64
+
+SCRATCH = {
+    "xb": ("sbuf", [128, 1040], "bfloat16"),
+    "usb": ("sbuf", [128, 32], "bfloat16"),
+    "usr": ("sbuf", [128, 512], "bfloat16"),
+    "zt": ("sbuf", [128, 4096], "bfloat16"),
+    "wf": ("sbuf", [128, 1536], "bfloat16"),
+    "hb": ("sbuf", [128, 512], "bfloat16"),
+    "mb": ("sbuf", [128, 1024], "bfloat16"),
+    "uq": ("sbuf", [128, 128], "float8_e4m3fn_x4"), "up": ("sbuf", [128, 128], "uint8"),
+    "xq": ("sbuf", [128, 256], "float8_e4m3fn_x4"), "xp": ("sbuf", [128, 256], "uint8"),
+    "hq": ("sbuf", [128, 128], "float8_e4m3fn_x4"), "hp": ("sbuf", [128, 128], "uint8"),
+    "mq": ("sbuf", [128, 256], "float8_e4m3fn_x4"), "mp": ("sbuf", [128, 256], "uint8"),
+    "wfq": ("sbuf", [128, 384], "float8_e4m3fn_x4"), "wfp": ("sbuf", [128, 384], "uint8"),
+    "wq": ("sbuf", [128, 3072], "float8_e4m3fn_x4"), "wp": ("sbuf", [128, 3072], "uint8"),
+    "lc": ("sbuf", [128, 320], "float8_e4m3fn_x4"), "lp": ("sbuf", [128, 320], "uint8"),
+    "ia": ("sbuf", [128, 32], "float32"),
+    "pidx": ("sbuf", [128, 1], "int32"),
+    "pci": ("sbuf", [128, 3], "int32"),
+    "pcf": ("sbuf", [128, 4], "float32"),
+    "n16": ("sbuf", [128, 256], "float32"),
+    "mk": ("sbuf", [128, 256], "float32"),
+    "rst": ("sbuf", [128, 256], "float32"),
+    "n4": ("sbuf", [128, 64], "float32"),
+    "mk4": ("sbuf", [128, 64], "float32"),
+    "rst4": ("sbuf", [128, 64], "float32"),
+    "oi": ("sbuf", [128, 16], "int32"),
+    "oj": ("sbuf", [128, 16], "int32"),
+    "tc65": ("sbuf", [128, 16], "float32"),
+    "tc64": ("sbuf", [128, 16], "float32"),
+    "j4": ("sbuf", [128, 256], "float32"),
+    "im": ("sbuf", [128, 16], "float32"),
+    "mj": ("sbuf", [128, 16], "float32"),
+    "c96": ("sbuf", [128, 96], "float32"),
+    "rk": ("sbuf", [128, 96], "float32"),
+    "ul": ("sbuf", [128, 32], "uint16"),
+    "sm": ("sbuf", [128, 256], "float32"),
+    "sc": ("sbuf", [128, 256], "float32"),
+    "srep": ("sbuf", [128, 96], "float32"),
+    "sl": ("sbuf", [128, 96], "float32"),
+    "ga": ("sbuf", [128, 96], "float32"),
+    "gb": ("sbuf", [128, 48], "float32"),
+    "gc16": ("sbuf", [128, 16], "float32"),
+    "eo": ("sbuf", [128, 16], "float32"),
+    "xo": ("sbuf", [128, 32], "float32"),
+    "cop": ("sbuf", [128, 40], "float32"),
+    "exo": ("sbuf", [128, 32], "float32"),
+    "bto": ("sbuf", [128, 32], "float32"),
+    "n1": ("sbuf", [128, 16], "float32"),
+    "n2": ("sbuf", [128, 16], "float32"),
+    "zz": ("sbuf", [128, 16], "float32"),
+    "offu": ("sbuf", [128, 16], "uint16"),
+    "wd": ("sbuf", [128, 384], "float32"),
+    "wm": ("sbuf", [128, 64], "float32"),
+    "ws": ("sbuf", [128, 64], "float32"),
+    "cl": ("sbuf", [128, 16], "uint16"),
+    "n3": ("sbuf", [128, 16], "float32"),
+    "ml": ("sbuf", [128, 64], "uint16"),
+    "m1": ("sbuf", [128, 48], "float32"),
+    "c1": ("sbuf", [128, 48], "float32"),
+    "m01": ("sbuf", [128, 16], "float32"),
+    "m12": ("sbuf", [128, 16], "float32"),
+    "c2": ("sbuf", [128, 16], "float32"),
+    "aa": ("sbuf", [128, 48], "float32"),
+    "ee": ("sbuf", [128, 96], "float32"),
+    "cs": ("sbuf", [128, 96], "float32"),
+    "ctp": ("sbuf", [128, 104], "float32"),
+    "ex": ("sbuf", [128, 96], "float32"),
+    "bt": ("sbuf", [128, 96], "float32"),
+    "eb": ("sbuf", [128, 96], "float32"),
+    "kk": ("sbuf", [128, 96], "float32"),
+    "ke": ("sbuf", [128, 96], "float32"),
+    "t48": ("sbuf", [128, 48], "float32"),
+    "t16": ("sbuf", [128, 16], "float32"),
+    "x32": ("sbuf", [128, 32], "float32"),
+    "xt": ("sbuf", [128, 32], "float32"),
+    "xx": ("sbuf", [128, 64], "float32"),
+    "xr": ("sbuf", [128, 64], "float32"),
+    "ru": ("sbuf", [128, 64], "uint16"),
+    "lst": ("sbuf", [128, 256], "uint16"),
+    "we": ("sbuf", [128, 96], "float32"),
+    "w48": ("sbuf", [128, 48], "float32"),
+    "w16": ("sbuf", [128, 16], "float32"),
+    "x33": ("sbuf", [128, 32], "float32"),
+    "wt": ("sbuf", [128, 32], "float32"),
+    "pw": ("sbuf", [128, NP * PW], "float32"),
+    "acc": ("sbuf", [128, 768], "float32"),
+}
+for _b in range(8):
+    SCRATCH["ps%d" % _b] = ("psum", [128, 512], "float32")
+
+SEMAPHORES = ["sv", "ss", "st", "sg", "dx", "du", "dw0", "dw1", "dw2", "dwf", "rs", "rc", "ls", "dn", "dy"] + ["dl%d" % _a for _a in range(4)]
+
+ADD, SUB, MUL = AluOpType.add, AluOpType.subtract, AluOpType.mult
+MAX, GT, GE, EQ = AluOpType.max, AluOpType.is_gt, AluOpType.is_ge, AluOpType.is_equal
+COPY = ActivationFunctionType.Copy
+
+
+def rank_program(g, core, T, topo):
+    r = T.rank_of(core)
+    if r is None:
+        return
+    N = len(T.cores)
+    others = [s for s in range(N) if s != r]
+    order = [s for s in range(N) if s % 2 == 0] + [s for s in range(N) if s % 2 == 1]
+
+    queues = {"g": g, "v": g.vector, "s": g.scalar, "t": g.tensor, "y": g.sync}
+    V, S, TE, Y = g.vector, g.scalar, g.tensor, g.sync
+    count = {"sv": 0, "ss": 0, "st": 0, "sg": 0}
+    seen = {}
+
+    def wait(q, sem, n):
+        if n > seen.get((q, sem), 0):
+            queues[q].wait_ge(T.sem[sem], n)
+            seen[(q, sem)] = n
+
+    def done(sem, ins):
+        ins.then_inc(T.sem[sem], 1)
+        count[sem] += 1
+        return count[sem]
+
+    def v(ins):
+        return done("sv", ins)
+
+    def s_(ins):
+        return done("ss", ins)
+
+    def t_(ins):
+        return done("st", ins)
+
+    def vw(n):
+        wait("v", "sv", n)
+
+    Y.dma_start(T.xb[:, 0:1024], T.x[:, :]).then_inc(T.sem.dx, 16)
+    S.dma_start(T.usb[:, :], T.us[:, 0:32]).then_inc(T.sem.du, 16)
+
+    def iota(out, pattern, base=0, cm=0, flag=True):
+        if flag:
+            return done("sg", g.iota(out, pattern, base, cm, allow_small_or_imprecise_dtypes=True))
+        return done("sg", g.iota(out, pattern, base, cm))
+
+    i_p = iota(T.pidx[:, :], [[1, 1]], 0, 1, False)
+    i_a = iota(T.ia[:, :], [[4, 8], [0, 4]])
+    i_n16 = iota(T.n16[:, :], [[0, 16], [1, 16]])
+    i_o = iota(T.oi[:, :], [[1, 16]], 0, 16, False)
+    i_n4 = iota(T.n4[:, :], [[0, 16], [1, 4]])
+    i_j4 = iota(T.j4[:, :], [[4, 256]])
+    i_m = iota(T.im[:, :], [[64, 16]], -1024)
+    i_c0 = iota(T.c96[:, :], [[0, 96]])
+    wait("g", "sg", i_c0)
+    for e, s in enumerate(order):
+        slot = others.index(s) if s != r else N - 1
+        i_c = iota(T.c96[:, 16 * e:16 * e + 1], [[1, 1]], CAP * slot - 1)
+    i_rk = iota(T.rk[:, :], [[1, 2], [2, 3], [0, 16]])
+
+    wait("v", "sg", i_p)
+    a = v(V.tensor_scalar(T.pci[:, 0:1], T.pidx[:, :], 15, None, AluOpType.bitwise_and))
+    a = v(V.tensor_scalar(T.pci[:, 1:2], T.pidx[:, :], 3, None, AluOpType.bitwise_and))
+    a = v(V.tensor_scalar(T.pci[:, 2:3], T.pidx[:, :], 2, 3, AluOpType.logical_shift_right, AluOpType.bitwise_and))
+    vw(a)
+    c_p = v(V.tensor_copy(T.pcf[:, 0:3], T.pci[:, :]))
+    vw(c_p)
+    wait("v", "sg", i_a)
+    c_ul = v(V.tensor_scalar(T.ul[:, :], T.ia[:, :], T.pcf[:, 1:2], None, ADD))
+    wait("v", "sg", i_n16)
+    c_mk = v(V.tensor_scalar(T.mk[:, :], T.n16[:, :], T.pcf[:, 0:1], None, EQ))
+    c_rst = v(V.tensor_scalar(T.rst[:, :], T.n16[:, :], 0.0, None, GT))
+    c_x0 = v(V.memset(T.xb[:, 1024:1040], 0.0))
+    wait("v", "du", 16)
+    vw(c_ul)
+    c_u = v(V.tensor_copy(T.usr[:, 0:256], T.usb[:, 0:32].indirect(T.ul[:, 0:16])))
+    wait("s", "du", 16)
+    wait("s", "sv", c_ul)
+    s_u = s_(S.activation(T.usr[:, 256:512], T.usb[:, 0:32].indirect(T.ul[:, 16:32]), COPY))
+    c_z = v(V.memset(T.zt[:, :], 0.0))
+    vw(c_u)
+    wait("v", "ss", s_u)
+    c_uq = v(V.quantize_mx(T.uq[:, :], T.up[:, :], T.usr[:, :]))
+    wait("v", "dx", 16)
+    c_xq = v(V.quantize_mx(T.xq[:, :], T.xp[:, :], T.xb[:, 0:1024]))
+
+    def load_w(o):
+        for h in range(8):
+            Y.dma_start(T.zt[16 * h:16 * h + 16, 512 * h:512 * h + 512],
+                        T.w[16 * h:16 * h + 16, 512 * o:512 * o + 512]).then_inc(T.sem["dw%d" % o], 16)
+
+    wait("y", "dx", 16)
+    wait("y", "sv", c_z)
+    load_w(0)
+    Y.dma_start(T.wf[:, :], T.w[:, :]).then_inc(T.sem.dwf, 16)
+
+    wait("t", "sv", c_xq)
+    p_s = t_(TE.matmul_mx(T.ps0[:, 0:256], T.uq[:, 0:128], T.up[:, 0:128], T.xq[:, 0:256], T.xp[:, 0:256], True, True))
+    wait("v", "st", p_s)
+    vw(c_rst)
+    a = v(V.tensor_tensor(T.sm[:, :], T.ps0[:, 0:256], T.mk[:, :], MUL))
+    c_ps0 = a
+    vw(a)
+    a = v(V.tensor_tensor_scan(T.sc[:, :], T.rst[:, :], T.sm[:, :], 0.0, MUL, ADD))
+    vw(a)
+    c_so = v(V.tensor_copy(T.srep[:, 0:16], T.sc[:, 15:256:16]))
+
+    dst_ids, emask = [], None
+    for s in others:
+        rid, pid, _se = topo.addr(T.cores[s])
+        dst_ids.append(DstId(rid=rid, pnc=pid))
+        m = topo.mask(core, T.cores[s])
+        emask = m if emask is None else emask & m
+    ne = len([b for b in range(16) if emask >> b & 1])
+
+    def send(src, dsts, sem):
+        g.remote_dma_fused([RemoteDMATransfer(dst_ids=dst_ids, dma_engine_mask=emask, remote_sem=T.sem[sem],
+                                              srcs=[src], dsts=dsts)], local_sem=T.sem.ls)
+
+    e0 = order.index(r)
+    wait("g", "sv", c_so)
+    send(T.srep[:, 0:16], [T.sl[:, 16 * e0:16 * e0 + 16] for _s in others], "rs")
+
+    vw(c_so)
+    a = v(V.tensor_copy(T.sl[:, 16 * e0:16 * e0 + 16], T.srep[:, 0:16]))
+    a = v(V.tensor_copy(T.srep[:, 16:32], T.srep[:, 0:16]))
+    vw(a)
+    v(V.tensor_copy(T.srep[:, 32:64], T.srep[:, 0:32]))
+    c_rep = v(V.tensor_copy(T.srep[:, 64:96], T.srep[:, 0:32]))
+    v(V.memset(T.hb[:, 256:512], 0.0))
+    v(V.memset(T.wd[:, 0:64], 0.0))
+    v(V.memset(T.xo[:, 16:32], 0.0))
+    v(V.memset(T.cop[:, 0:1], 0.0))
+    v(V.memset(T.ctp[:, 0:1], 0.0))
+    v(V.memset(T.x32[:, 16:32], 0.0))
+    v(V.memset(T.x33[:, 16:32], 0.0))
+    wait("v", "sg", i_rk)
+    v(V.tensor_scalar(T.mk4[:, :], T.n4[:, :], T.pcf[:, 2:3], None, EQ))
+    v(V.tensor_scalar(T.rst4[:, :], T.n4[:, :], 0.0, None, GT))
+    v(V.tensor_scalar(T.pcf[:, 3:4], T.pcf[:, 0:1], 4.0, None, MUL))
+    a = v(V.tensor_scalar(T.oj[:, :], T.oi[:, :], 255, None, AluOpType.bitwise_and))
+    vw(a)
+    v(V.tensor_scalar(T.tc65[:, :], T.oj[:, :], 65.0, None, ADD))
+    v(V.tensor_scalar(T.tc64[:, :], T.oj[:, :], 64.0, None, ADD))
+    c_cst = v(V.tensor_scalar(T.mj[:, :], T.im[:, :], T.pcf[:, 3:4], None, ADD))
+
+    def quant_w(o):
+        wait("v", "dw%d" % o, 128)
+        for k in range(2):
+            c = v(V.quantize_mx(T.wq[:, 1024 * o + 512 * k:1024 * o + 512 * k + 512],
+                                T.wp[:, 1024 * o + 512 * k:1024 * o + 512 * k + 512],
+                                T.zt[:, 2048 * k:2048 * k + 2048]))
+        return c
+
+    c_w = [quant_w(0)]
+    wait("y", "sv", c_w[0])
+    load_w(1)
+    wait("v", "dwf", 16)
+    c_wf = v(V.quantize_mx(T.wfq[:, :], T.wfp[:, :], T.wf[:, :]))
+    for k in range(NP):
+        c_p0 = v(V.memset(T.pw[:, PW * k + 320:PW * k + PW], 0.0))
+
+    wait("v", "rs", ne * len(others))
+    vw(c_cst)
+    runs = []
+    for e, s in enumerate(order):
+        op = GT if s < r else GE
+        if runs and runs[-1][2] is op:
+            runs[-1][1] = e + 1
+        else:
+            runs.append([e, e + 1, op])
+    for b, e, op in runs:
+        a = v(V.tensor_tensor(T.ga[:, 16 * b:16 * e], T.srep[:, 16 * b:16 * e], T.sl[:, 16 * b:16 * e], op))
+    vw(a)
+    a = v(V.tensor_tensor(T.gb[:, :], T.ga[:, 0:48], T.ga[:, 48:96], MUL))
+    vw(a)
+    a = v(V.tensor_tensor(T.gc16[:, :], T.gb[:, 0:16], T.gb[:, 16:32], MUL))
+    vw(a)
+    c_eo = v(V.tensor_tensor(T.eo[:, :], T.gc16[:, :], T.gb[:, 32:48], MUL))
+    vw(c_eo)
+    c_co = v(V.tensor_tensor_scan(T.xo[:, 0:16], T.rst[:, 0:16], T.eo[:, :], 0.0, MUL, ADD))
+    c_n1 = v(V.tensor_tensor(T.n1[:, :], T.eo[:, :], T.tc65[:, :], MUL))
+    vw(c_co)
+    a = v(V.transpose(T.cop[:, 1:33], T.xo[:, :]))
+    vw(c_n1)
+    c_n2 = v(V.tensor_tensor(T.n2[:, :], T.tc64[:, :], T.n1[:, :], SUB))
+    vw(a)
+    a = v(V.tensor_tensor_scan(T.exo[:, :], T.cop[:, 0:32], T.rst[:, 0:32], 0.0, ADD, MUL))
+    vw(c_n2)
+    c_zz = v(V.tensor_tensor(T.zz[:, :], T.xo[:, 0:16], T.n2[:, :], ADD))
+    vw(a)
+    a = v(V.transpose(T.bto[:, :], T.exo[:, :]))
+    vw(a)
+    a = v(V.tensor_scalar(T.offu[:, :], T.zz[:, :], T.bto[:, 15:16], None, ADD))
+    vw(a)
+    a = v(V.tensor_copy(T.wd[:, 0:384].indirect(T.offu[:, 0:16]), T.j4[:, :]))
+    vw(a)
+    a = v(V.tensor_tensor(T.wm[:, :], T.wd[:, 0:64], T.mk4[:, :], MUL))
+    vw(a)
+    a = v(V.tensor_tensor_scan(T.ws[:, :], T.rst4[:, :], T.wm[:, :], 0.0, MUL, ADD))
+    vw(a)
+    c_cl = v(V.tensor_scalar(T.cl[:, :], T.ws[:, 3:64:4], T.pcf[:, 1:2], None, ADD))
+    wait("s", "sv", c_cl)
+    wait("s", "dx", 16)
+    s_h = s_(S.activation(T.hb[:, 128:256], T.xb[:, 0:1040].indirect(T.cl[:, 8:16]), COPY))
+    vw(c_cl)
+    a = v(V.tensor_copy(T.hb[:, 0:128], T.xb[:, 0:1040].indirect(T.cl[:, 0:8])))
+    vw(a)
+    wait("v", "ss", s_h)
+    c_hq = v(V.quantize_mx(T.hq[:, :], T.hp[:, :], T.hb[:, :]))
+    wait("g", "sv", c_hq)
+    lands = []
+    for s in others:
+        k = [q for q in range(N) if q != s].index(r)
+        lands.append((CAP * k, CAP * k + CAP))
+    send(T.hq[:, 0:CAP].bitcast(dt.uint8), [T.lc[:, b:e].bitcast(dt.uint8) for b, e in lands], "rc")
+    send(T.hp[:, 0:CAP], [T.lp[:, b:e] for b, e in lands], "rc")
+
+    a = v(V.tensor_tensor(T.n3[:, :], T.eo[:, :], T.mj[:, :], MUL))
+    vw(a)
+    for t in range(4):
+        c_ml = v(V.tensor_scalar(T.ml[:, 16 * t:16 * t + 16], T.n3[:, :], 1024.0 + t, None, ADD))
+    wait("s", "sv", c_ml)
+    for t in range(4):
+        s_m = s_(S.activation(T.mb[:, t:1024:4], T.xb[:, 0:1040].indirect(T.ml[:, 16 * t:16 * t + 16]), COPY))
+
+    v(V.tensor_tensor(T.m1[:, :], T.sl[:, 0:48], T.sl[:, 48:96], MAX))
+    a = v(V.tensor_tensor(T.c1[:, :], T.sl[:, 48:96], T.sl[:, 0:48], GT))
+    vw(a)
+    v(V.tensor_tensor(T.m01[:, :], T.m1[:, 0:16], T.m1[:, 16:32], MAX))
+    v(V.tensor_tensor(T.m12[:, :], T.m1[:, 16:32], T.m1[:, 32:48], MAX))
+    a = v(V.tensor_tensor(T.c2[:, :], T.m1[:, 16:32], T.m1[:, 0:16], GT))
+    vw(a)
+    a45 = v(V.tensor_tensor(T.aa[:, 32:48], T.m1[:, 32:48], T.m01[:, :], GT))
+    v(V.tensor_tensor(T.aa[:, 0:16], T.m1[:, 0:16], T.m12[:, :], GE))
+    vw(a45)
+    a = v(V.tensor_tensor(T.aa[:, 16:32], T.c2[:, :], T.aa[:, 32:48], GT))
+    vw(a)
+    a = v(V.tensor_tensor(T.ee[:, 48:96], T.aa[:, :], T.c1[:, :], MUL))
+    vw(a)
+    a = v(V.tensor_tensor(T.ee[:, 0:48], T.aa[:, :], T.ee[:, 48:96], SUB))
+    vw(a)
+    c_cs = v(V.tensor_tensor_scan(T.cs[:, :], T.rst[:, 0:96], T.ee[:, :], 0.0, MUL, ADD))
+    c_eb = v(V.tensor_tensor(T.eb[:, :], T.ee[:, :], T.c96[:, :], ADD))
+    vw(c_cs)
+    a = v(V.transpose(T.ctp[:, 1:97], T.cs[:, :]))
+    vw(a)
+    a = v(V.tensor_tensor_scan(T.ex[:, :], T.ctp[:, 0:96], T.rst[:, 0:96], 0.0, ADD, MUL))
+    vw(a)
+    a = v(V.transpose(T.bt[:, :], T.ex[:, :]))
+    vw(a)
+    a = v(V.tensor_tensor(T.eb[:, 0:96:16], T.eb[:, 0:96:16], T.bt[:, 15:96:16], ADD))
+    vw(a)
+    a = v(V.tensor_tensor_scan(T.kk[:, :], T.rst[:, 0:96], T.eb[:, :], 0.0, MUL, ADD))
+    vw(a)
+    a = v(V.tensor_tensor(T.ke[:, :], T.kk[:, :], T.ee[:, :], MUL))
+    vw(a)
+    a = v(V.tensor_tensor(T.t48[:, :], T.ke[:, 0:48], T.ke[:, 48:96], ADD))
+    vw(a)
+    a = v(V.tensor_tensor(T.t16[:, :], T.t48[:, 0:16], T.t48[:, 16:32], ADD))
+    vw(a)
+    a = v(V.tensor_tensor(T.x32[:, 0:16], T.t16[:, :], T.t48[:, 32:48], ADD))
+    vw(a)
+    a = v(V.transpose(T.xt[:, :], T.x32[:, :]))
+    vw(a)
+    for d in range(2):
+        for h in range(2):
+            a = v(V.tensor_copy(T.xx[:, 32 * d + 16 * h:32 * d + 16 * h + 16], T.xt[:, 16 * d:16 * d + 16]))
+    vw(a)
+    a = v(V.transpose(T.xr[:, :], T.xx[:, :]))
+    vw(a)
+    c_ru = v(V.tensor_copy(T.ru[:, :], T.xr[:, :]))
+    for k in range(4):
+        for b in range(4):
+            q = "y" if b % 2 == 0 else "s"
+            wait(q, "sv", c_ru)
+            queues[q].dma_start(T.lst[32 * b:32 * b + 32, 64 * k:64 * k + 64],
+                                T.ru[32 * k:32 * k + 32, :]).then_inc(T.sem["dl%d" % k], 16)
+
+    wait("v", "ss", s_m)
+    c_mq = v(V.quantize_mx(T.mq[:, :], T.mp[:, :], T.mb[:, :]))
+    wait("t", "sv", c_mq)
+    bank_free = [("sv", c_ps0)] + [None] * 7
+    p_m = []
+    for o in range(3):
+        p_m.append(t_(TE.matmul_mx(T["ps%d" % (1 + o)][:, 0:256], T.wfq[:, 128 * o:128 * o + 128],
+                                   T.wfp[:, 128 * o:128 * o + 128], T.mq[:, 0:256], T.mp[:, 0:256], True, True)))
+    s_acc = []
+    for o in range(3):
+        wait("s", "st", p_m[o])
+        s_acc.append(s_(S.activation(T.acc[:, 256 * o:256 * o + 256], T["ps%d" % (1 + o)][:, 0:256], COPY)))
+        bank_free[1 + o] = ("ss", s_acc[o])
+
+    c_w.append(quant_w(1))
+    wait("y", "sv", c_w[1])
+    load_w(2)
+
+    a = v(V.tensor_tensor(T.we[:, :], T.ee[:, :], T.rk[:, :], MUL))
+    vw(a)
+    a = v(V.tensor_tensor(T.w48[:, :], T.we[:, 0:48], T.we[:, 48:96], ADD))
+    vw(a)
+    a = v(V.tensor_tensor(T.w16[:, :], T.w48[:, 0:16], T.w48[:, 16:32], ADD))
+    vw(a)
+    a = v(V.tensor_tensor(T.x33[:, 0:16], T.w16[:, :], T.w48[:, 32:48], ADD))
+    vw(a)
+    c_wt = v(V.transpose(T.wt[:, :], T.x33[:, :]))
+    wait("y", "sv", c_wt)
+    for k in range(4):
+        for h in range(2):
+            Y.dma_start(T.wn[2 * k + h:2 * k + h + 1, :],
+                        T.wt[32 * k:32 * k + 16, 16 * h:16 * h + 16]).then_inc(T.sem.dn, 16)
+
+    wait("t", "rc", 2 * ne * len(others))
+    gath = {}
+    wait("s", "sv", c_p0)
+    for o in range(3):
+        if o == 1:
+            c_w.append(quant_w(2))
+        for h in range(8):
+            n = 8 * o + h
+            b = n % 8
+            wait("t", "sv", c_w[o])
+            if bank_free[b] is not None:
+                wait("t", *bank_free[b])
+            k = 1024 * o + 128 * h
+            p = t_(TE.matmul_mx(T["ps%d" % b][:, 0:320], T.wq[:, k:k + 128], T.wp[:, k:k + 128],
+                                T.lc[:, 0:320], T.lp[:, 0:320], True, True))
+            w0 = PW * (n % NP)
+            if n >= NP:
+                wait("s", "sv", gath[n - NP])
+            wait("s", "st", p)
+            c = s_(S.activation(T.pw[:, w0:w0 + 320], T["ps%d" % b][:, 0:320], COPY))
+            bank_free[b] = ("ss", c)
+            wait("v", "ss", c)
+            wait("v", "dl%d" % (h // 2), 64)
+            vw(gath.get(n - 1, 0) if h else 0)
+            acc = T.acc[:, 256 * o:256 * o + 256]
+            gath[n] = v(V.tensor_tensor(acc, T.pw[:, w0:w0 + PW].indirect(T.lst[:, 32 * h:32 * h + 16]), acc, ADD))
+        wait("y", "sv", gath[8 * o + 7])
+        Y.dma_start(T.y[:, 256 * o:256 * o + 256], T.acc[:, 256 * o:256 * o + 256]).then_inc(T.sem.dy, 16)
+
+    wait("y", "dy", 48)
+    wait("y", "dn", 128)
+    wait("g", "ls", 3 * ne)
+    for sem in ("sv", "ss", "st", "sg"):
+        wait("g", sem, count[sem])

@@ -5,99 +5,32 @@ NP = 8
 PW = 384
 CAP = 64
 
-SCRATCH = {
-    "xb": ("sbuf", [128, 1040], "bfloat16"),
-    "usb": ("sbuf", [128, 32], "bfloat16"),
-    "usr": ("sbuf", [128, 512], "bfloat16"),
-    "zt": ("sbuf", [128, 4096], "bfloat16"),
-    "wf": ("sbuf", [128, 1536], "bfloat16"),
-    "hb": ("sbuf", [128, 512], "bfloat16"),
-    "mb": ("sbuf", [128, 1024], "bfloat16"),
-    "uq": ("sbuf", [128, 128], "float8_e4m3fn_x4"), "up": ("sbuf", [128, 128], "uint8"),
-    "xq": ("sbuf", [128, 256], "float8_e4m3fn_x4"), "xp": ("sbuf", [128, 256], "uint8"),
-    "hq": ("sbuf", [128, 128], "float8_e4m3fn_x4"), "hp": ("sbuf", [128, 128], "uint8"),
-    "mq": ("sbuf", [128, 256], "float8_e4m3fn_x4"), "mp": ("sbuf", [128, 256], "uint8"),
-    "wfq": ("sbuf", [128, 384], "float8_e4m3fn_x4"), "wfp": ("sbuf", [128, 384], "uint8"),
-    "wq": ("sbuf", [128, 3072], "float8_e4m3fn_x4"), "wp": ("sbuf", [128, 3072], "uint8"),
-    "lc": ("sbuf", [128, 320], "float8_e4m3fn_x4"), "lp": ("sbuf", [128, 320], "uint8"),
-    "ia": ("sbuf", [128, 32], "float32"),
-    "pidx": ("sbuf", [128, 1], "int32"),
-    "pci": ("sbuf", [128, 3], "int32"),
-    "pcf": ("sbuf", [128, 4], "float32"),
-    "n16": ("sbuf", [128, 256], "float32"),
-    "mk": ("sbuf", [128, 256], "float32"),
-    "rst": ("sbuf", [128, 256], "float32"),
-    "n4": ("sbuf", [128, 64], "float32"),
-    "mk4": ("sbuf", [128, 64], "float32"),
-    "rst4": ("sbuf", [128, 64], "float32"),
-    "oi": ("sbuf", [128, 16], "int32"),
-    "oj": ("sbuf", [128, 16], "int32"),
-    "tc65": ("sbuf", [128, 16], "float32"),
-    "tc64": ("sbuf", [128, 16], "float32"),
-    "j4": ("sbuf", [128, 256], "float32"),
-    "im": ("sbuf", [128, 16], "float32"),
-    "mj": ("sbuf", [128, 16], "float32"),
-    "c96": ("sbuf", [128, 96], "float32"),
-    "rk": ("sbuf", [128, 96], "float32"),
-    "ul": ("sbuf", [128, 32], "uint16"),
-    "sm": ("sbuf", [128, 256], "float32"),
-    "sc": ("sbuf", [128, 256], "float32"),
-    "srep": ("sbuf", [128, 96], "float32"),
-    "sl": ("sbuf", [128, 96], "float32"),
-    "ga": ("sbuf", [128, 96], "float32"),
-    "gb": ("sbuf", [128, 48], "float32"),
-    "gc16": ("sbuf", [128, 16], "float32"),
-    "eo": ("sbuf", [128, 16], "float32"),
-    "xo": ("sbuf", [128, 32], "float32"),
-    "cop": ("sbuf", [128, 40], "float32"),
-    "exo": ("sbuf", [128, 32], "float32"),
-    "bto": ("sbuf", [128, 32], "float32"),
-    "n1": ("sbuf", [128, 16], "float32"),
-    "n2": ("sbuf", [128, 16], "float32"),
-    "zz": ("sbuf", [128, 16], "float32"),
-    "offu": ("sbuf", [128, 16], "uint16"),
-    "wd": ("sbuf", [128, 384], "float32"),
-    "wm": ("sbuf", [128, 64], "float32"),
-    "ws": ("sbuf", [128, 64], "float32"),
-    "cl": ("sbuf", [128, 16], "uint16"),
-    "n3": ("sbuf", [128, 16], "float32"),
-    "ml": ("sbuf", [128, 64], "uint16"),
-    "m1": ("sbuf", [128, 48], "float32"),
-    "c1": ("sbuf", [128, 48], "float32"),
-    "m01": ("sbuf", [128, 16], "float32"),
-    "m12": ("sbuf", [128, 16], "float32"),
-    "c2": ("sbuf", [128, 16], "float32"),
-    "aa": ("sbuf", [128, 48], "float32"),
-    "ee": ("sbuf", [128, 96], "float32"),
-    "cs": ("sbuf", [128, 96], "float32"),
-    "ctp": ("sbuf", [128, 104], "float32"),
-    "ex": ("sbuf", [128, 96], "float32"),
-    "bt": ("sbuf", [128, 96], "float32"),
-    "eb": ("sbuf", [128, 96], "float32"),
-    "kk": ("sbuf", [128, 96], "float32"),
-    "ke": ("sbuf", [128, 96], "float32"),
-    "t48": ("sbuf", [128, 48], "float32"),
-    "t16": ("sbuf", [128, 16], "float32"),
-    "x32": ("sbuf", [128, 32], "float32"),
-    "xt": ("sbuf", [128, 32], "float32"),
-    "xx": ("sbuf", [128, 64], "float32"),
-    "xr": ("sbuf", [128, 64], "float32"),
-    "ru": ("sbuf", [128, 64], "uint16"),
-    "lst": ("sbuf", [128, 256], "uint16"),
-    "we": ("sbuf", [128, 96], "float32"),
-    "w48": ("sbuf", [128, 48], "float32"),
-    "w16": ("sbuf", [128, 16], "float32"),
-    "x33": ("sbuf", [128, 32], "float32"),
-    "wt": ("sbuf", [128, 32], "float32"),
-    "pw": ("sbuf", [128, NP * PW], "float32"),
-    "acc": ("sbuf", [128, 768], "float32"),
-}
+SCRATCH = {}
+
+
+def _bufs(dtype, names):
+    for item in names.split():
+        name, width = item.split(":")
+        SCRATCH[name] = ("sbuf", [128, int(width)], dtype)
+
+
+_bufs("bfloat16", "xb:1040 usb:32 usr:512 zt:8192 zb:1024 wf:1536 hb:512 mb:1024 n16:256 mk:256 rst:256")
+_bufs("float8_e4m3fn_x4", "uq:128 xq:256 hq:128 mq:256 wfq:384 wq:3072 lc:320")
+_bufs("uint8", "up:128 xp:256 hp:128 mp:256 wfp:384 wp:3072 lp:320")
+_bufs("int32", "pidx:1 pci:3 oi:16 oj:16")
+_bufs("uint16", "ul:32 offu:16 cl:16 ml:64 ru:64 lst:256")
+_bufs("float32", "ia:32 pcf:4 n4:64 mk4:64 rst4:64 tc65:16 tc64:16 j4:256 im:16 mj:16 c96:96 rk:96")
+_bufs("float32", "sm:256 sc:256 srep:16 sl:96 ga:96 eo:16 xo:32 cop:40 exo:32 bto:32 n1:16 n2:16 zz:16 wd:384 wm:64 ws:64 n3:16")
+_bufs("float32", "m1:48 c1:48 m01:16 m12:16 c2:16 aa:48 ee:96 cs:96 ctp:104 ex:96 bt:96 eb:96 kk:96 ke:96 t48:48 t16:16 x32:32 xt:32 xx:64 xr:64")
+_bufs("float32", "we:96 w48:48 w16:16 x33:32 wt:32 acc:768")
+_bufs("float32", "pw:%d" % (NP * PW))
 for _b in range(8):
     SCRATCH["ps%d" % _b] = ("psum", [128, 512], "float32")
 
-SEMAPHORES = ["sv", "ss", "st", "sg", "dx", "du", "dw0", "dw1", "dw2", "dwf", "rs", "rc", "ls", "dn", "dy"] + ["dl%d" % _a for _a in range(4)]
+SEMAPHORES = ["sv", "ss", "st", "sg", "dx", "du", "dwf", "rc", "ls", "dn", "dy"]
+SEMAPHORES += ["dl%d" % _a for _a in range(4)] + ["dw%d" % _a for _a in range(6)] + ["rs%d" % _a for _a in range(6)]
 
-ADD, SUB, MUL = AluOpType.add, AluOpType.subtract, AluOpType.mult
+ADD, SUB, MUL, AND = AluOpType.add, AluOpType.subtract, AluOpType.mult, AluOpType.bitwise_and
 MAX, GT, GE, EQ = AluOpType.max, AluOpType.is_gt, AluOpType.is_ge, AluOpType.is_equal
 COPY = ActivationFunctionType.Copy
 
@@ -137,8 +70,14 @@ def rank_program(g, core, T, topo):
     def vw(n):
         wait("v", "sv", n)
 
-    Y.dma_start(T.xb[:, 0:1024], T.x[:, :]).then_inc(T.sem.dx, 16)
+    def tt(out, a, b, op):
+        return v(V.tensor_tensor(out, a, b, op))
+
+    def ts(out, a, scalar, op):
+        return v(V.tensor_scalar(out, a, scalar, None, op))
+
     S.dma_start(T.usb[:, :], T.us[:, 0:32]).then_inc(T.sem.du, 16)
+    Y.dma_start(T.xb[:, 0:1024], T.x[:, :]).then_inc(T.sem.dx, 16)
 
     def iota(out, pattern, base=0, cm=0, flag=True):
         if flag:
@@ -148,66 +87,83 @@ def rank_program(g, core, T, topo):
     i_p = iota(T.pidx[:, :], [[1, 1]], 0, 1, False)
     i_a = iota(T.ia[:, :], [[4, 8], [0, 4]])
     i_n16 = iota(T.n16[:, :], [[0, 16], [1, 16]])
-    i_o = iota(T.oi[:, :], [[1, 16]], 0, 16, False)
-    i_n4 = iota(T.n4[:, :], [[0, 16], [1, 4]])
+    iota(T.oi[:, :], [[1, 16]], 0, 16, False)
+    iota(T.n4[:, :], [[0, 16], [1, 4]])
+    iota(T.im[:, :], [[64, 16]], -1024)
     i_j4 = iota(T.j4[:, :], [[4, 256]])
-    i_m = iota(T.im[:, :], [[64, 16]], -1024)
     i_c0 = iota(T.c96[:, :], [[0, 96]])
     wait("g", "sg", i_c0)
     for e, s in enumerate(order):
         slot = others.index(s) if s != r else N - 1
-        i_c = iota(T.c96[:, 16 * e:16 * e + 1], [[1, 1]], CAP * slot - 1)
-    i_rk = iota(T.rk[:, :], [[1, 2], [2, 3], [0, 16]])
+        iota(T.c96[:, 16 * e:16 * e + 1], [[1, 1]], CAP * slot - 1)
 
     wait("v", "sg", i_p)
-    a = v(V.tensor_scalar(T.pci[:, 0:1], T.pidx[:, :], 15, None, AluOpType.bitwise_and))
-    a = v(V.tensor_scalar(T.pci[:, 1:2], T.pidx[:, :], 3, None, AluOpType.bitwise_and))
-    a = v(V.tensor_scalar(T.pci[:, 2:3], T.pidx[:, :], 2, 3, AluOpType.logical_shift_right, AluOpType.bitwise_and))
+    ts(T.pci[:, 1:2], T.pidx[:, :], 3, AND)
+    ts(T.pci[:, 0:1], T.pidx[:, :], 15, AND)
+    a = v(V.tensor_scalar(T.pci[:, 2:3], T.pidx[:, :], 2, 3, AluOpType.logical_shift_right, AND))
     vw(a)
-    c_p = v(V.tensor_copy(T.pcf[:, 0:3], T.pci[:, :]))
-    vw(c_p)
+    a = v(V.tensor_copy(T.pcf[:, 0:3], T.pci[:, :]))
+    vw(a)
     wait("v", "sg", i_a)
-    c_ul = v(V.tensor_scalar(T.ul[:, :], T.ia[:, :], T.pcf[:, 1:2], None, ADD))
-    wait("v", "sg", i_n16)
-    c_mk = v(V.tensor_scalar(T.mk[:, :], T.n16[:, :], T.pcf[:, 0:1], None, EQ))
-    c_rst = v(V.tensor_scalar(T.rst[:, :], T.n16[:, :], 0.0, None, GT))
-    c_x0 = v(V.memset(T.xb[:, 1024:1040], 0.0))
+    c_ul = ts(T.ul[:, :], T.ia[:, :], T.pcf[:, 1:2], ADD)
+    c_zb = v(V.memset(T.zb[:, :], 0.0))
+    c_z0 = v(V.memset(T.zt[:, 0:2048], 0.0))
     wait("v", "du", 16)
     vw(c_ul)
     c_u = v(V.tensor_copy(T.usr[:, 0:256], T.usb[:, 0:32].indirect(T.ul[:, 0:16])))
     wait("s", "du", 16)
     wait("s", "sv", c_ul)
     s_u = s_(S.activation(T.usr[:, 256:512], T.usb[:, 0:32].indirect(T.ul[:, 16:32]), COPY))
-    c_z = v(V.memset(T.zt[:, :], 0.0))
+    v(V.memset(T.xb[:, 1024:1040], 0.0))
+    wait("v", "sg", i_n16)
+    ts(T.rst[:, :], T.n16[:, :], 0.0, GT)
+    wait("s", "sv", c_zb)
+    s_z = [s_(S.activation(T.zt[:, 2048 + 1024 * k:3072 + 1024 * k], T.zb[:, :], COPY)) for k in range(6)]
     vw(c_u)
     wait("v", "ss", s_u)
-    c_uq = v(V.quantize_mx(T.uq[:, :], T.up[:, :], T.usr[:, :]))
+    v(V.quantize_mx(T.uq[:, :], T.up[:, :], T.usr[:, :]))
     wait("v", "dx", 16)
     c_xq = v(V.quantize_mx(T.xq[:, :], T.xp[:, :], T.xb[:, 0:1024]))
+    c_mk = ts(T.mk[:, :], T.n16[:, :], T.pcf[:, 0:1], EQ)
 
-    def load_w(o):
-        for h in range(8):
-            Y.dma_start(T.zt[16 * h:16 * h + 16, 512 * h:512 * h + 512],
-                        T.w[16 * h:16 * h + 16, 512 * o:512 * o + 512]).then_inc(T.sem["dw%d" % o], 16)
+    place = [0, 2048, 4096, 6144, 0, 2048]
+
+    def load_w(c):
+        o, f = c // 2, 4 * (c % 2)
+        for h in range(f, f + 4):
+            z = place[c] + 512 * (h - f)
+            Y.dma_start(T.zt[16 * h:16 * h + 16, z:z + 512],
+                        T.w[16 * h:16 * h + 16, 512 * o:512 * o + 512]).then_inc(T.sem["dw%d" % c], 16)
+
+    c_w = {}
+
+    def quant_w(c):
+        wait("v", "dw%d" % c, 64)
+        c_w[c] = v(V.quantize_mx(T.wq[:, 512 * c:512 * c + 512], T.wp[:, 512 * c:512 * c + 512],
+                                 T.zt[:, place[c]:place[c] + 2048]))
 
     wait("y", "dx", 16)
-    wait("y", "sv", c_z)
+    wait("y", "sv", c_z0)
     load_w(0)
+    wait("y", "ss", s_z[1])
+    load_w(1)
     Y.dma_start(T.wf[:, :], T.w[:, :]).then_inc(T.sem.dwf, 16)
+    wait("y", "ss", s_z[3])
+    load_w(2)
 
     wait("t", "sv", c_xq)
     p_s = t_(TE.matmul_mx(T.ps0[:, 0:256], T.uq[:, 0:128], T.up[:, 0:128], T.xq[:, 0:256], T.xp[:, 0:256], True, True))
     wait("v", "st", p_s)
-    vw(c_rst)
-    a = v(V.tensor_tensor(T.sm[:, :], T.ps0[:, 0:256], T.mk[:, :], MUL))
-    c_ps0 = a
-    vw(a)
+    vw(c_mk)
+    c_ps0 = tt(T.sm[:, :], T.ps0[:, 0:256], T.mk[:, :], MUL)
+    vw(c_ps0)
     a = v(V.tensor_tensor_scan(T.sc[:, :], T.rst[:, :], T.sm[:, :], 0.0, MUL, ADD))
     vw(a)
     c_so = v(V.tensor_copy(T.srep[:, 0:16], T.sc[:, 15:256:16]))
 
+    turn = [(r + k) % N for k in range(1, N)]
     dst_ids, emask = [], None
-    for s in others:
+    for s in turn:
         rid, pid, _se = topo.addr(T.cores[s])
         dst_ids.append(DstId(rid=rid, pnc=pid))
         m = topo.mask(core, T.cores[s])
@@ -220,87 +176,74 @@ def rank_program(g, core, T, topo):
 
     e0 = order.index(r)
     wait("g", "sv", c_so)
-    send(T.srep[:, 0:16], [T.sl[:, 16 * e0:16 * e0 + 16] for _s in others], "rs")
+    send(T.srep[:, 0:16], [T.sl[:, 16 * e0:16 * e0 + 16] for _s in turn], "rs%d" % r)
+
+    iota(T.xo[:, 16:32], [[0, 16]])
+    iota(T.cop[:, 0:1], [[0, 1]])
+    i_z1 = iota(T.wd[:, 0:64], [[0, 64]])
+    iota(T.ctp[:, 0:1], [[0, 1]])
+    iota(T.x32[:, 16:32], [[0, 16]])
+    iota(T.x33[:, 16:32], [[0, 16]])
+    i_rk = iota(T.rk[:, :], [[1, 2], [2, 3], [0, 16]])
 
     vw(c_so)
-    a = v(V.tensor_copy(T.sl[:, 16 * e0:16 * e0 + 16], T.srep[:, 0:16]))
-    a = v(V.tensor_copy(T.srep[:, 16:32], T.srep[:, 0:16]))
-    vw(a)
-    v(V.tensor_copy(T.srep[:, 32:64], T.srep[:, 0:32]))
-    c_rep = v(V.tensor_copy(T.srep[:, 64:96], T.srep[:, 0:32]))
+    v(V.tensor_copy(T.sl[:, 16 * e0:16 * e0 + 16], T.srep[:, 0:16]))
     v(V.memset(T.hb[:, 256:512], 0.0))
-    v(V.memset(T.wd[:, 0:64], 0.0))
-    v(V.memset(T.xo[:, 16:32], 0.0))
-    v(V.memset(T.cop[:, 0:1], 0.0))
-    v(V.memset(T.ctp[:, 0:1], 0.0))
-    v(V.memset(T.x32[:, 16:32], 0.0))
-    v(V.memset(T.x33[:, 16:32], 0.0))
-    wait("v", "sg", i_rk)
-    v(V.tensor_scalar(T.mk4[:, :], T.n4[:, :], T.pcf[:, 2:3], None, EQ))
-    v(V.tensor_scalar(T.rst4[:, :], T.n4[:, :], 0.0, None, GT))
-    v(V.tensor_scalar(T.pcf[:, 3:4], T.pcf[:, 0:1], 4.0, None, MUL))
-    a = v(V.tensor_scalar(T.oj[:, :], T.oi[:, :], 255, None, AluOpType.bitwise_and))
+    wait("v", "sg", i_j4)
+    ts(T.mk4[:, :], T.n4[:, :], T.pcf[:, 2:3], EQ)
+    ts(T.rst4[:, :], T.n4[:, :], 0.0, GT)
+    ts(T.oj[:, :], T.oi[:, :], 255, AND)
+    a = ts(T.pcf[:, 3:4], T.pcf[:, 0:1], 4.0, MUL)
     vw(a)
-    v(V.tensor_scalar(T.tc65[:, :], T.oj[:, :], 65.0, None, ADD))
-    v(V.tensor_scalar(T.tc64[:, :], T.oj[:, :], 64.0, None, ADD))
-    c_cst = v(V.tensor_scalar(T.mj[:, :], T.im[:, :], T.pcf[:, 3:4], None, ADD))
-
-    def quant_w(o):
-        wait("v", "dw%d" % o, 128)
-        for k in range(2):
-            c = v(V.quantize_mx(T.wq[:, 1024 * o + 512 * k:1024 * o + 512 * k + 512],
-                                T.wp[:, 1024 * o + 512 * k:1024 * o + 512 * k + 512],
-                                T.zt[:, 2048 * k:2048 * k + 2048]))
-        return c
-
-    c_w = [quant_w(0)]
+    ts(T.tc65[:, :], T.oj[:, :], 65.0, ADD)
+    ts(T.tc64[:, :], T.oj[:, :], 64.0, ADD)
+    c_cst = ts(T.mj[:, :], T.im[:, :], T.pcf[:, 3:4], ADD)
+    quant_w(0)
     wait("y", "sv", c_w[0])
-    load_w(1)
-    wait("v", "dwf", 16)
-    c_wf = v(V.quantize_mx(T.wfq[:, :], T.wfp[:, :], T.wf[:, :]))
-    for k in range(NP):
-        c_p0 = v(V.memset(T.pw[:, PW * k + 320:PW * k + PW], 0.0))
+    load_w(4)
+    wait("y", "ss", s_z[5])
+    load_w(3)
+    quant_w(1)
+    wait("y", "sv", c_w[1])
+    load_w(5)
 
-    wait("v", "rs", ne * len(others))
+    wait("v", "sg", i_z1)
     vw(c_cst)
-    runs = []
-    for e, s in enumerate(order):
+    c_eo = None
+    for s in reversed(turn):
+        wait("v", "rs%d" % s, ne)
+        e = order.index(s)
         op = GT if s < r else GE
-        if runs and runs[-1][2] is op:
-            runs[-1][1] = e + 1
+        if c_eo is None:
+            c_eo = tt(T.eo[:, :], T.srep[:, 0:16], T.sl[:, 16 * e:16 * e + 16], op)
         else:
-            runs.append([e, e + 1, op])
-    for b, e, op in runs:
-        a = v(V.tensor_tensor(T.ga[:, 16 * b:16 * e], T.srep[:, 16 * b:16 * e], T.sl[:, 16 * b:16 * e], op))
-    vw(a)
-    a = v(V.tensor_tensor(T.gb[:, :], T.ga[:, 0:48], T.ga[:, 48:96], MUL))
-    vw(a)
-    a = v(V.tensor_tensor(T.gc16[:, :], T.gb[:, 0:16], T.gb[:, 16:32], MUL))
-    vw(a)
-    c_eo = v(V.tensor_tensor(T.eo[:, :], T.gc16[:, :], T.gb[:, 32:48], MUL))
+            k = 16 * turn.index(s)
+            a = tt(T.ga[:, k:k + 16], T.srep[:, 0:16], T.sl[:, 16 * e:16 * e + 16], op)
+            vw(a)
+            c_eo = tt(T.eo[:, :], T.eo[:, :], T.ga[:, k:k + 16], MUL)
     vw(c_eo)
     c_co = v(V.tensor_tensor_scan(T.xo[:, 0:16], T.rst[:, 0:16], T.eo[:, :], 0.0, MUL, ADD))
-    c_n1 = v(V.tensor_tensor(T.n1[:, :], T.eo[:, :], T.tc65[:, :], MUL))
+    c_n1 = tt(T.n1[:, :], T.eo[:, :], T.tc65[:, :], MUL)
     vw(c_co)
     a = v(V.transpose(T.cop[:, 1:33], T.xo[:, :]))
     vw(c_n1)
-    c_n2 = v(V.tensor_tensor(T.n2[:, :], T.tc64[:, :], T.n1[:, :], SUB))
+    c_n2 = tt(T.n2[:, :], T.tc64[:, :], T.n1[:, :], SUB)
     vw(a)
     a = v(V.tensor_tensor_scan(T.exo[:, :], T.cop[:, 0:32], T.rst[:, 0:32], 0.0, ADD, MUL))
     vw(c_n2)
-    c_zz = v(V.tensor_tensor(T.zz[:, :], T.xo[:, 0:16], T.n2[:, :], ADD))
+    tt(T.zz[:, :], T.xo[:, 0:16], T.n2[:, :], ADD)
     vw(a)
     a = v(V.transpose(T.bto[:, :], T.exo[:, :]))
     vw(a)
-    a = v(V.tensor_scalar(T.offu[:, :], T.zz[:, :], T.bto[:, 15:16], None, ADD))
+    a = ts(T.offu[:, :], T.zz[:, :], T.bto[:, 15:16], ADD)
     vw(a)
     a = v(V.tensor_copy(T.wd[:, 0:384].indirect(T.offu[:, 0:16]), T.j4[:, :]))
     vw(a)
-    a = v(V.tensor_tensor(T.wm[:, :], T.wd[:, 0:64], T.mk4[:, :], MUL))
+    a = tt(T.wm[:, :], T.wd[:, 0:64], T.mk4[:, :], MUL)
     vw(a)
     a = v(V.tensor_tensor_scan(T.ws[:, :], T.rst4[:, :], T.wm[:, :], 0.0, MUL, ADD))
     vw(a)
-    c_cl = v(V.tensor_scalar(T.cl[:, :], T.ws[:, 3:64:4], T.pcf[:, 1:2], None, ADD))
+    c_cl = ts(T.cl[:, :], T.ws[:, 3:64:4], T.pcf[:, 1:2], ADD)
     wait("s", "sv", c_cl)
     wait("s", "dx", 16)
     s_h = s_(S.activation(T.hb[:, 128:256], T.xb[:, 0:1040].indirect(T.cl[:, 8:16]), COPY))
@@ -311,56 +254,59 @@ def rank_program(g, core, T, topo):
     c_hq = v(V.quantize_mx(T.hq[:, :], T.hp[:, :], T.hb[:, :]))
     wait("g", "sv", c_hq)
     lands = []
-    for s in others:
+    for s in turn:
         k = [q for q in range(N) if q != s].index(r)
         lands.append((CAP * k, CAP * k + CAP))
     send(T.hq[:, 0:CAP].bitcast(dt.uint8), [T.lc[:, b:e].bitcast(dt.uint8) for b, e in lands], "rc")
     send(T.hp[:, 0:CAP], [T.lp[:, b:e] for b, e in lands], "rc")
+    for k in range(NP):
+        i_p0 = iota(T.pw[:, PW * k + 320:PW * k + PW], [[0, 64]])
 
-    a = v(V.tensor_tensor(T.n3[:, :], T.eo[:, :], T.mj[:, :], MUL))
+    a = tt(T.n3[:, :], T.eo[:, :], T.mj[:, :], MUL)
     vw(a)
     for t in range(4):
-        c_ml = v(V.tensor_scalar(T.ml[:, 16 * t:16 * t + 16], T.n3[:, :], 1024.0 + t, None, ADD))
+        c_ml = ts(T.ml[:, 16 * t:16 * t + 16], T.n3[:, :], 1024.0 + t, ADD)
     wait("s", "sv", c_ml)
     for t in range(4):
         s_m = s_(S.activation(T.mb[:, t:1024:4], T.xb[:, 0:1040].indirect(T.ml[:, 16 * t:16 * t + 16]), COPY))
 
-    v(V.tensor_tensor(T.m1[:, :], T.sl[:, 0:48], T.sl[:, 48:96], MAX))
-    a = v(V.tensor_tensor(T.c1[:, :], T.sl[:, 48:96], T.sl[:, 0:48], GT))
+    tt(T.m1[:, :], T.sl[:, 0:48], T.sl[:, 48:96], MAX)
+    a = tt(T.c1[:, :], T.sl[:, 48:96], T.sl[:, 0:48], GT)
     vw(a)
-    v(V.tensor_tensor(T.m01[:, :], T.m1[:, 0:16], T.m1[:, 16:32], MAX))
-    v(V.tensor_tensor(T.m12[:, :], T.m1[:, 16:32], T.m1[:, 32:48], MAX))
-    a = v(V.tensor_tensor(T.c2[:, :], T.m1[:, 16:32], T.m1[:, 0:16], GT))
+    tt(T.m01[:, :], T.m1[:, 0:16], T.m1[:, 16:32], MAX)
+    tt(T.m12[:, :], T.m1[:, 16:32], T.m1[:, 32:48], MAX)
+    a = tt(T.c2[:, :], T.m1[:, 16:32], T.m1[:, 0:16], GT)
     vw(a)
-    a45 = v(V.tensor_tensor(T.aa[:, 32:48], T.m1[:, 32:48], T.m01[:, :], GT))
-    v(V.tensor_tensor(T.aa[:, 0:16], T.m1[:, 0:16], T.m12[:, :], GE))
+    a45 = tt(T.aa[:, 32:48], T.m1[:, 32:48], T.m01[:, :], GT)
+    tt(T.aa[:, 0:16], T.m1[:, 0:16], T.m12[:, :], GE)
     vw(a45)
-    a = v(V.tensor_tensor(T.aa[:, 16:32], T.c2[:, :], T.aa[:, 32:48], GT))
+    a = tt(T.aa[:, 16:32], T.c2[:, :], T.aa[:, 32:48], GT)
     vw(a)
-    a = v(V.tensor_tensor(T.ee[:, 48:96], T.aa[:, :], T.c1[:, :], MUL))
+    a = tt(T.ee[:, 48:96], T.aa[:, :], T.c1[:, :], MUL)
     vw(a)
-    a = v(V.tensor_tensor(T.ee[:, 0:48], T.aa[:, :], T.ee[:, 48:96], SUB))
+    a = tt(T.ee[:, 0:48], T.aa[:, :], T.ee[:, 48:96], SUB)
     vw(a)
-    c_cs = v(V.tensor_tensor_scan(T.cs[:, :], T.rst[:, 0:96], T.ee[:, :], 0.0, MUL, ADD))
-    c_eb = v(V.tensor_tensor(T.eb[:, :], T.ee[:, :], T.c96[:, :], ADD))
-    vw(c_cs)
+    a = v(V.tensor_tensor_scan(T.cs[:, :], T.rst[:, 0:96], T.ee[:, :], 0.0, MUL, ADD))
+    wait("v", "sg", i_rk)
+    tt(T.eb[:, :], T.ee[:, :], T.c96[:, :], ADD)
+    vw(a)
     a = v(V.transpose(T.ctp[:, 1:97], T.cs[:, :]))
     vw(a)
     a = v(V.tensor_tensor_scan(T.ex[:, :], T.ctp[:, 0:96], T.rst[:, 0:96], 0.0, ADD, MUL))
     vw(a)
     a = v(V.transpose(T.bt[:, :], T.ex[:, :]))
     vw(a)
-    a = v(V.tensor_tensor(T.eb[:, 0:96:16], T.eb[:, 0:96:16], T.bt[:, 15:96:16], ADD))
+    a = tt(T.eb[:, 0:96:16], T.eb[:, 0:96:16], T.bt[:, 15:96:16], ADD)
     vw(a)
     a = v(V.tensor_tensor_scan(T.kk[:, :], T.rst[:, 0:96], T.eb[:, :], 0.0, MUL, ADD))
     vw(a)
-    a = v(V.tensor_tensor(T.ke[:, :], T.kk[:, :], T.ee[:, :], MUL))
+    a = tt(T.ke[:, :], T.kk[:, :], T.ee[:, :], MUL)
     vw(a)
-    a = v(V.tensor_tensor(T.t48[:, :], T.ke[:, 0:48], T.ke[:, 48:96], ADD))
+    a = tt(T.t48[:, :], T.ke[:, 0:48], T.ke[:, 48:96], ADD)
     vw(a)
-    a = v(V.tensor_tensor(T.t16[:, :], T.t48[:, 0:16], T.t48[:, 16:32], ADD))
+    a = tt(T.t16[:, :], T.t48[:, 0:16], T.t48[:, 16:32], ADD)
     vw(a)
-    a = v(V.tensor_tensor(T.x32[:, 0:16], T.t16[:, :], T.t48[:, 32:48], ADD))
+    a = tt(T.x32[:, 0:16], T.t16[:, :], T.t48[:, 32:48], ADD)
     vw(a)
     a = v(V.transpose(T.xt[:, :], T.x32[:, :]))
     vw(a)
@@ -378,31 +324,29 @@ def rank_program(g, core, T, topo):
             queues[q].dma_start(T.lst[32 * b:32 * b + 32, 64 * k:64 * k + 64],
                                 T.ru[32 * k:32 * k + 32, :]).then_inc(T.sem["dl%d" % k], 16)
 
+    wait("v", "dwf", 16)
+    v(V.quantize_mx(T.wfq[:, :], T.wfp[:, :], T.wf[:, :]))
     wait("v", "ss", s_m)
     c_mq = v(V.quantize_mx(T.mq[:, :], T.mp[:, :], T.mb[:, :]))
     wait("t", "sv", c_mq)
     bank_free = [("sv", c_ps0)] + [None] * 7
-    p_m = []
-    for o in range(3):
-        p_m.append(t_(TE.matmul_mx(T["ps%d" % (1 + o)][:, 0:256], T.wfq[:, 128 * o:128 * o + 128],
-                                   T.wfp[:, 128 * o:128 * o + 128], T.mq[:, 0:256], T.mp[:, 0:256], True, True)))
-    s_acc = []
+    p_m = [t_(TE.matmul_mx(T["ps%d" % (1 + o)][:, 0:256], T.wfq[:, 128 * o:128 * o + 128],
+                           T.wfp[:, 128 * o:128 * o + 128], T.mq[:, 0:256], T.mp[:, 0:256], True, True)) for o in range(3)]
     for o in range(3):
         wait("s", "st", p_m[o])
-        s_acc.append(s_(S.activation(T.acc[:, 256 * o:256 * o + 256], T["ps%d" % (1 + o)][:, 0:256], COPY)))
-        bank_free[1 + o] = ("ss", s_acc[o])
+        bank_free[1 + o] = ("ss", s_(S.activation(T.acc[:, 256 * o:256 * o + 256], T["ps%d" % (1 + o)][:, 0:256], COPY)))
 
-    c_w.append(quant_w(1))
-    wait("y", "sv", c_w[1])
-    load_w(2)
-
-    a = v(V.tensor_tensor(T.we[:, :], T.ee[:, :], T.rk[:, :], MUL))
+    a = tt(T.we[:, :], T.ee[:, :], T.rk[:, :], MUL)
+    quant_w(2)
     vw(a)
-    a = v(V.tensor_tensor(T.w48[:, :], T.we[:, 0:48], T.we[:, 48:96], ADD))
+    a = tt(T.w48[:, :], T.we[:, 0:48], T.we[:, 48:96], ADD)
+    quant_w(3)
     vw(a)
-    a = v(V.tensor_tensor(T.w16[:, :], T.w48[:, 0:16], T.w48[:, 16:32], ADD))
+    a = tt(T.w16[:, :], T.w48[:, 0:16], T.w48[:, 16:32], ADD)
+    quant_w(4)
     vw(a)
-    a = v(V.tensor_tensor(T.x33[:, 0:16], T.w16[:, :], T.w48[:, 32:48], ADD))
+    a = tt(T.x33[:, 0:16], T.w16[:, :], T.w48[:, 32:48], ADD)
+    quant_w(5)
     vw(a)
     c_wt = v(V.transpose(T.wt[:, :], T.x33[:, :]))
     wait("y", "sv", c_wt)
@@ -412,35 +356,38 @@ def rank_program(g, core, T, topo):
                         T.wt[32 * k:32 * k + 16, 16 * h:16 * h + 16]).then_inc(T.sem.dn, 16)
 
     wait("t", "rc", 2 * ne * len(others))
-    gath = {}
-    wait("s", "sv", c_p0)
-    for o in range(3):
-        if o == 1:
-            c_w.append(quant_w(2))
-        for h in range(8):
-            n = 8 * o + h
-            b = n % 8
-            wait("t", "sv", c_w[o])
-            if bank_free[b] is not None:
-                wait("t", *bank_free[b])
-            k = 1024 * o + 128 * h
-            p = t_(TE.matmul_mx(T["ps%d" % b][:, 0:320], T.wq[:, k:k + 128], T.wp[:, k:k + 128],
-                                T.lc[:, 0:320], T.lp[:, 0:320], True, True))
-            w0 = PW * (n % NP)
-            if n >= NP:
-                wait("s", "sv", gath[n - NP])
-            wait("s", "st", p)
-            c = s_(S.activation(T.pw[:, w0:w0 + 320], T["ps%d" % b][:, 0:320], COPY))
-            bank_free[b] = ("ss", c)
-            wait("v", "ss", c)
-            wait("v", "dl%d" % (h // 2), 64)
-            vw(gath.get(n - 1, 0) if h else 0)
-            acc = T.acc[:, 256 * o:256 * o + 256]
-            gath[n] = v(V.tensor_tensor(acc, T.pw[:, w0:w0 + PW].indirect(T.lst[:, 32 * h:32 * h + 16]), acc, ADD))
-        wait("y", "sv", gath[8 * o + 7])
-        Y.dma_start(T.y[:, 256 * o:256 * o + 256], T.acc[:, 256 * o:256 * o + 256]).then_inc(T.sem.dy, 16)
+    wait("v", "sg", i_p0)
+    items = [(o, h) for h in range(6) for o in (0, 1)]
+    items += [(0, 6), (2, 0), (0, 7), (2, 1), (1, 6), (2, 2), (1, 7), (2, 3), (2, 4), (2, 5), (2, 6), (2, 7)]
+    gath, last = [], {}
+    for n, (o, h) in enumerate(items):
+        bank = T["ps%d" % (n % 8)]
+        wait("t", "sv", c_w[2 * o + h // 4])
+        if bank_free[n % 8] is not None:
+            wait("t", *bank_free[n % 8])
+        w = 1024 * o + 128 * h
+        p = t_(TE.matmul_mx(bank[:, 0:320], T.wq[:, w:w + 128], T.wp[:, w:w + 128], T.lc[:, 0:320], T.lp[:, 0:320], True, True))
+        w0 = PW * (n % NP)
+        if n >= NP:
+            wait("s", "sv", gath[n - NP])
+        wait("s", "st", p)
+        c = s_(S.activation(T.pw[:, w0:w0 + 320], bank[:, 0:320], COPY))
+        bank_free[n % 8] = ("ss", c)
+        wait("v", "ss", c)
+        wait("v", "dl%d" % (h // 2), 64)
+        if o in last:
+            vw(last[o])
+        win = T.pw[:, w0:w0 + PW]
+        for f in range(2 if n == 23 else 1):
+            m = 8 if n == 23 else 16
+            acc = T.acc[:, 256 * o + 128 * f:256 * o + 128 * f + 16 * m]
+            last[o] = tt(acc, win.indirect(T.lst[:, 32 * h + 8 * f:32 * h + 8 * f + m]), acc, ADD)
+            if h == 7:
+                wait("y", "sv", last[o])
+                Y.dma_start(T.y[:, 256 * o + 128 * f:256 * o + 128 * f + 16 * m], acc).then_inc(T.sem.dy, 16)
+        gath.append(last[o])
 
-    wait("y", "dy", 48)
+    wait("y", "dy", 64)
     wait("y", "dn", 128)
     wait("g", "ls", 3 * ne)
     for sem in ("sv", "ss", "st", "sg"):

@@ -76,6 +76,9 @@ def rank_program(g, core, T, topo):
     def ts(out, a, scalar, op):
         return v(V.tensor_scalar(out, a, scalar, None, op))
 
+    def scan(out, a, b, op0, op1):
+        return v(V.tensor_tensor_scan(out, a, b, 0.0, op0, op1))
+
     S.dma_start(T.usb[:, :], T.us[:, 0:32]).then_inc(T.sem.du, 16)
     Y.dma_start(T.xb[:, 0:1024], T.x[:, :]).then_inc(T.sem.dx, 16)
 
@@ -101,20 +104,20 @@ def rank_program(g, core, T, topo):
     ts(T.pci[:, 1:2], T.pidx[:, :], 3, AND)
     ts(T.pci[:, 0:1], T.pidx[:, :], 15, AND)
     a = v(V.tensor_scalar(T.pci[:, 2:3], T.pidx[:, :], 2, 3, AluOpType.logical_shift_right, AND))
+    c_zb = v(V.memset(T.zb[:, :], 0.0))
     vw(a)
     a = v(V.tensor_copy(T.pcf[:, 0:3], T.pci[:, :]))
+    c_z0 = v(V.memset(T.zt[:, 0:2048], 0.0))
     vw(a)
     wait("v", "sg", i_a)
     c_ul = ts(T.ul[:, :], T.ia[:, :], T.pcf[:, 1:2], ADD)
-    c_zb = v(V.memset(T.zb[:, :], 0.0))
-    c_z0 = v(V.memset(T.zt[:, 0:2048], 0.0))
+    v(V.memset(T.xb[:, 1024:1040], 0.0))
     wait("v", "du", 16)
     vw(c_ul)
     c_u = v(V.tensor_copy(T.usr[:, 0:256], T.usb[:, 0:32].indirect(T.ul[:, 0:16])))
     wait("s", "du", 16)
     wait("s", "sv", c_ul)
     s_u = s_(S.activation(T.usr[:, 256:512], T.usb[:, 0:32].indirect(T.ul[:, 16:32]), COPY))
-    v(V.memset(T.xb[:, 1024:1040], 0.0))
     wait("v", "sg", i_n16)
     ts(T.rst[:, :], T.n16[:, :], 0.0, GT)
     wait("s", "sv", c_zb)
@@ -157,7 +160,7 @@ def rank_program(g, core, T, topo):
     vw(c_mk)
     c_ps0 = tt(T.sm[:, :], T.ps0[:, 0:256], T.mk[:, :], MUL)
     vw(c_ps0)
-    a = v(V.tensor_tensor_scan(T.sc[:, :], T.rst[:, :], T.sm[:, :], 0.0, MUL, ADD))
+    a = scan(T.sc[:, :], T.rst[:, :], T.sm[:, :], MUL, ADD)
     vw(a)
     c_so = v(V.tensor_copy(T.srep[:, 0:16], T.sc[:, 15:256:16]))
 
@@ -186,15 +189,14 @@ def rank_program(g, core, T, topo):
     iota(T.x33[:, 16:32], [[0, 16]])
     i_rk = iota(T.rk[:, :], [[1, 2], [2, 3], [0, 16]])
 
-    vw(c_so)
-    v(V.tensor_copy(T.sl[:, 16 * e0:16 * e0 + 16], T.srep[:, 0:16]))
-    v(V.memset(T.hb[:, 256:512], 0.0))
     wait("v", "sg", i_j4)
-    ts(T.mk4[:, :], T.n4[:, :], T.pcf[:, 2:3], EQ)
-    ts(T.rst4[:, :], T.n4[:, :], 0.0, GT)
     ts(T.oj[:, :], T.oi[:, :], 255, AND)
     a = ts(T.pcf[:, 3:4], T.pcf[:, 0:1], 4.0, MUL)
-    vw(a)
+    v(V.memset(T.hb[:, 256:512], 0.0))
+    ts(T.mk4[:, :], T.n4[:, :], T.pcf[:, 2:3], EQ)
+    ts(T.rst4[:, :], T.n4[:, :], 0.0, GT)
+    vw(max(a, c_so))
+    v(V.tensor_copy(T.sl[:, 16 * e0:16 * e0 + 16], T.srep[:, 0:16]))
     ts(T.tc65[:, :], T.oj[:, :], 65.0, ADD)
     ts(T.tc64[:, :], T.oj[:, :], 64.0, ADD)
     c_cst = ts(T.mj[:, :], T.im[:, :], T.pcf[:, 3:4], ADD)
@@ -206,6 +208,94 @@ def rank_program(g, core, T, topo):
     quant_w(1)
     wait("y", "sv", c_w[1])
     load_w(5)
+
+    at = {}
+
+    def r01():
+        tt(T.m1[:, :], T.sl[:, 0:48], T.sl[:, 48:96], MAX)
+        return tt(T.c1[:, :], T.sl[:, 48:96], T.sl[:, 0:48], GT)
+
+    def r02():
+        tt(T.m12[:, :], T.m1[:, 16:32], T.m1[:, 32:48], MAX)
+        tt(T.c2[:, :], T.m1[:, 16:32], T.m1[:, 0:16], GT)
+        return tt(T.m01[:, :], T.m1[:, 0:16], T.m1[:, 16:32], MAX)
+
+    def r03():
+        tt(T.aa[:, 0:16], T.m1[:, 0:16], T.m12[:, :], GE)
+        return tt(T.aa[:, 32:48], T.m1[:, 32:48], T.m01[:, :], GT)
+
+    def r04():
+        return tt(T.aa[:, 16:32], T.c2[:, :], T.aa[:, 32:48], GT)
+
+    def r05():
+        return tt(T.ee[:, 48:96], T.aa[:, :], T.c1[:, :], MUL)
+
+    def r06():
+        return tt(T.ee[:, 0:48], T.aa[:, :], T.ee[:, 48:96], SUB)
+
+    def r07():
+        a = scan(T.cs[:, :], T.rst[:, 0:96], T.ee[:, :], MUL, ADD)
+        wait("v", "sg", i_rk)
+        tt(T.eb[:, :], T.ee[:, :], T.c96[:, :], ADD)
+        return a
+
+    def r08():
+        return v(V.transpose(T.ctp[:, 1:97], T.cs[:, :]))
+
+    def r09():
+        return scan(T.ex[:, :], T.ctp[:, 0:96], T.rst[:, 0:96], ADD, MUL)
+
+    def r10():
+        return v(V.transpose(T.bt[:, :], T.ex[:, :]))
+
+    def r11():
+        return tt(T.eb[:, 0:96:16], T.eb[:, 0:96:16], T.bt[:, 15:96:16], ADD)
+
+    def r12():
+        return scan(T.kk[:, :], T.rst[:, 0:96], T.eb[:, :], MUL, ADD)
+
+    def r13():
+        return tt(T.ke[:, :], T.kk[:, :], T.ee[:, :], MUL)
+
+    def r14():
+        return tt(T.t48[:, :], T.ke[:, 0:48], T.ke[:, 48:96], ADD)
+
+    def r15():
+        return tt(T.t16[:, :], T.t48[:, 0:16], T.t48[:, 16:32], ADD)
+
+    def r16():
+        return tt(T.x32[:, 0:16], T.t16[:, :], T.t48[:, 32:48], ADD)
+
+    def r17():
+        return v(V.transpose(T.xt[:, :], T.x32[:, :]))
+
+    def r18():
+        for d in range(2):
+            for h in range(2):
+                a = v(V.tensor_copy(T.xx[:, 32 * d + 16 * h:32 * d + 16 * h + 16], T.xt[:, 16 * d:16 * d + 16]))
+        return a
+
+    def r19():
+        return v(V.transpose(T.xr[:, :], T.xx[:, :]))
+
+    def r20():
+        return v(V.tensor_copy(T.ru[:, :], T.xr[:, :]))
+
+    steps = [r01, r02, r03, r04, r05, r06, r07, r08, r09, r10, r11, r12, r13, r14, r15, r16, r17, r18, r19, r20]
+    own = []
+
+    def fill():
+        k = len(at)
+        if k < len(steps):
+            if k:
+                vw(at[k - 1])
+            at[k] = steps[k]()
+
+    def after(n):
+        own.append(n)
+        if len(own) % 2 == 1 or len(own) > 11:
+            fill()
+        vw(n)
 
     wait("v", "sg", i_z1)
     vw(c_cst)
@@ -221,35 +311,36 @@ def rank_program(g, core, T, topo):
             a = tt(T.ga[:, k:k + 16], T.srep[:, 0:16], T.sl[:, 16 * e:16 * e + 16], op)
             vw(a)
             c_eo = tt(T.eo[:, :], T.eo[:, :], T.ga[:, k:k + 16], MUL)
-    vw(c_eo)
-    c_co = v(V.tensor_tensor_scan(T.xo[:, 0:16], T.rst[:, 0:16], T.eo[:, :], 0.0, MUL, ADD))
+    after(c_eo)
+    c_co = scan(T.xo[:, 0:16], T.rst[:, 0:16], T.eo[:, :], MUL, ADD)
     c_n1 = tt(T.n1[:, :], T.eo[:, :], T.tc65[:, :], MUL)
-    vw(c_co)
+    after(c_co)
     a = v(V.transpose(T.cop[:, 1:33], T.xo[:, :]))
     vw(c_n1)
     c_n2 = tt(T.n2[:, :], T.tc64[:, :], T.n1[:, :], SUB)
-    vw(a)
-    a = v(V.tensor_tensor_scan(T.exo[:, :], T.cop[:, 0:32], T.rst[:, 0:32], 0.0, ADD, MUL))
+    after(a)
+    a = scan(T.exo[:, :], T.cop[:, 0:32], T.rst[:, 0:32], ADD, MUL)
     vw(c_n2)
     tt(T.zz[:, :], T.xo[:, 0:16], T.n2[:, :], ADD)
-    vw(a)
+    after(a)
     a = v(V.transpose(T.bto[:, :], T.exo[:, :]))
-    vw(a)
+    after(a)
     a = ts(T.offu[:, :], T.zz[:, :], T.bto[:, 15:16], ADD)
-    vw(a)
+    after(a)
     a = v(V.tensor_copy(T.wd[:, 0:384].indirect(T.offu[:, 0:16]), T.j4[:, :]))
-    vw(a)
+    after(a)
     a = tt(T.wm[:, :], T.wd[:, 0:64], T.mk4[:, :], MUL)
-    vw(a)
-    a = v(V.tensor_tensor_scan(T.ws[:, :], T.rst4[:, :], T.wm[:, :], 0.0, MUL, ADD))
-    vw(a)
+    after(a)
+    a = scan(T.ws[:, :], T.rst4[:, :], T.wm[:, :], MUL, ADD)
+    after(a)
     c_cl = ts(T.cl[:, :], T.ws[:, 3:64:4], T.pcf[:, 1:2], ADD)
     wait("s", "sv", c_cl)
     wait("s", "dx", 16)
     s_h = s_(S.activation(T.hb[:, 128:256], T.xb[:, 0:1040].indirect(T.cl[:, 8:16]), COPY))
-    vw(c_cl)
+    after(c_cl)
     a = v(V.tensor_copy(T.hb[:, 0:128], T.xb[:, 0:1040].indirect(T.cl[:, 0:8])))
-    vw(a)
+    c_n3 = tt(T.n3[:, :], T.eo[:, :], T.mj[:, :], MUL)
+    after(a)
     wait("v", "ss", s_h)
     c_hq = v(V.quantize_mx(T.hq[:, :], T.hp[:, :], T.hb[:, :]))
     wait("g", "sv", c_hq)
@@ -262,67 +353,38 @@ def rank_program(g, core, T, topo):
     for k in range(NP):
         i_p0 = iota(T.pw[:, PW * k + 320:PW * k + PW], [[0, 64]])
 
-    a = tt(T.n3[:, :], T.eo[:, :], T.mj[:, :], MUL)
-    vw(a)
+    vw(c_n3)
     for t in range(4):
         c_ml = ts(T.ml[:, 16 * t:16 * t + 16], T.n3[:, :], 1024.0 + t, ADD)
     wait("s", "sv", c_ml)
     for t in range(4):
         s_m = s_(S.activation(T.mb[:, t:1024:4], T.xb[:, 0:1040].indirect(T.ml[:, 16 * t:16 * t + 16]), COPY))
-
-    tt(T.m1[:, :], T.sl[:, 0:48], T.sl[:, 48:96], MAX)
-    a = tt(T.c1[:, :], T.sl[:, 48:96], T.sl[:, 0:48], GT)
-    vw(a)
-    tt(T.m01[:, :], T.m1[:, 0:16], T.m1[:, 16:32], MAX)
-    tt(T.m12[:, :], T.m1[:, 16:32], T.m1[:, 32:48], MAX)
-    a = tt(T.c2[:, :], T.m1[:, 16:32], T.m1[:, 0:16], GT)
-    vw(a)
-    a45 = tt(T.aa[:, 32:48], T.m1[:, 32:48], T.m01[:, :], GT)
-    tt(T.aa[:, 0:16], T.m1[:, 0:16], T.m12[:, :], GE)
-    vw(a45)
-    a = tt(T.aa[:, 16:32], T.c2[:, :], T.aa[:, 32:48], GT)
-    vw(a)
-    a = tt(T.ee[:, 48:96], T.aa[:, :], T.c1[:, :], MUL)
-    vw(a)
-    a = tt(T.ee[:, 0:48], T.aa[:, :], T.ee[:, 48:96], SUB)
-    vw(a)
-    a = v(V.tensor_tensor_scan(T.cs[:, :], T.rst[:, 0:96], T.ee[:, :], 0.0, MUL, ADD))
-    wait("v", "sg", i_rk)
-    tt(T.eb[:, :], T.ee[:, :], T.c96[:, :], ADD)
-    vw(a)
-    a = v(V.transpose(T.ctp[:, 1:97], T.cs[:, :]))
-    vw(a)
-    a = v(V.tensor_tensor_scan(T.ex[:, :], T.ctp[:, 0:96], T.rst[:, 0:96], 0.0, ADD, MUL))
-    vw(a)
-    a = v(V.transpose(T.bt[:, :], T.ex[:, :]))
-    vw(a)
-    a = tt(T.eb[:, 0:96:16], T.eb[:, 0:96:16], T.bt[:, 15:96:16], ADD)
-    vw(a)
-    a = v(V.tensor_tensor_scan(T.kk[:, :], T.rst[:, 0:96], T.eb[:, :], 0.0, MUL, ADD))
-    vw(a)
-    a = tt(T.ke[:, :], T.kk[:, :], T.ee[:, :], MUL)
-    vw(a)
-    a = tt(T.t48[:, :], T.ke[:, 0:48], T.ke[:, 48:96], ADD)
-    vw(a)
-    a = tt(T.t16[:, :], T.t48[:, 0:16], T.t48[:, 16:32], ADD)
-    vw(a)
-    a = tt(T.x32[:, 0:16], T.t16[:, :], T.t48[:, 32:48], ADD)
-    vw(a)
-    a = v(V.transpose(T.xt[:, :], T.x32[:, :]))
-    vw(a)
-    for d in range(2):
-        for h in range(2):
-            a = v(V.tensor_copy(T.xx[:, 32 * d + 16 * h:32 * d + 16 * h + 16], T.xt[:, 16 * d:16 * d + 16]))
-    vw(a)
-    a = v(V.transpose(T.xr[:, :], T.xx[:, :]))
-    vw(a)
-    c_ru = v(V.tensor_copy(T.ru[:, :], T.xr[:, :]))
+    while len(at) < 7:
+        fill()
+    vw(at[5])
+    a = tt(T.we[:, :], T.ee[:, :], T.rk[:, :], MUL)
+    after(a)
+    a = tt(T.w48[:, :], T.we[:, 0:48], T.we[:, 48:96], ADD)
+    after(a)
+    a = tt(T.w16[:, :], T.w48[:, 0:16], T.w48[:, 16:32], ADD)
+    after(a)
+    a = tt(T.x33[:, 0:16], T.w16[:, :], T.w48[:, 32:48], ADD)
+    after(a)
+    c_wt = v(V.transpose(T.wt[:, :], T.x33[:, :]))
+    while len(at) < len(steps):
+        fill()
+    c_ru = at[len(steps) - 1]
     for k in range(4):
         for b in range(4):
             q = "y" if b % 2 == 0 else "s"
             wait(q, "sv", c_ru)
             queues[q].dma_start(T.lst[32 * b:32 * b + 32, 64 * k:64 * k + 64],
                                 T.ru[32 * k:32 * k + 32, :]).then_inc(T.sem["dl%d" % k], 16)
+    wait("y", "sv", c_wt)
+    for k in range(4):
+        for h in range(2):
+            Y.dma_start(T.wn[2 * k + h:2 * k + h + 1, :],
+                        T.wt[32 * k:32 * k + 16, 16 * h:16 * h + 16]).then_inc(T.sem.dn, 16)
 
     wait("v", "dwf", 16)
     v(V.quantize_mx(T.wfq[:, :], T.wfp[:, :], T.wf[:, :]))
@@ -335,30 +397,13 @@ def rank_program(g, core, T, topo):
     for o in range(3):
         wait("s", "st", p_m[o])
         bank_free[1 + o] = ("ss", s_(S.activation(T.acc[:, 256 * o:256 * o + 256], T["ps%d" % (1 + o)][:, 0:256], COPY)))
-
-    a = tt(T.we[:, :], T.ee[:, :], T.rk[:, :], MUL)
-    quant_w(2)
-    vw(a)
-    a = tt(T.w48[:, :], T.we[:, 0:48], T.we[:, 48:96], ADD)
-    quant_w(3)
-    vw(a)
-    a = tt(T.w16[:, :], T.w48[:, 0:16], T.w48[:, 16:32], ADD)
-    quant_w(4)
-    vw(a)
-    a = tt(T.x33[:, 0:16], T.w16[:, :], T.w48[:, 32:48], ADD)
-    quant_w(5)
-    vw(a)
-    c_wt = v(V.transpose(T.wt[:, :], T.x33[:, :]))
-    wait("y", "sv", c_wt)
-    for k in range(4):
-        for h in range(2):
-            Y.dma_start(T.wn[2 * k + h:2 * k + h + 1, :],
-                        T.wt[32 * k:32 * k + 16, 16 * h:16 * h + 16]).then_inc(T.sem.dn, 16)
+    for c in range(2, 6):
+        quant_w(c)
 
     wait("t", "rc", 2 * ne * len(others))
     wait("v", "sg", i_p0)
-    items = [(o, h) for h in range(6) for o in (0, 1)]
-    items += [(0, 6), (2, 0), (0, 7), (2, 1), (1, 6), (2, 2), (1, 7), (2, 3), (2, 4), (2, 5), (2, 6), (2, 7)]
+    items = [(o, h) for h in range(5) for o in (0, 1)]
+    items += [(0, 5), (2, 0), (0, 6), (2, 1), (0, 7), (2, 2), (1, 5), (2, 3), (1, 6), (2, 4), (1, 7), (2, 5), (2, 6), (2, 7)]
     gath, last = [], {}
     for n, (o, h) in enumerate(items):
         bank = T["ps%d" % (n % 8)]
@@ -375,17 +420,18 @@ def rank_program(g, core, T, topo):
         bank_free[n % 8] = ("ss", c)
         wait("v", "ss", c)
         wait("v", "dl%d" % (h // 2), 64)
-        if o in last:
-            vw(last[o])
         win = T.pw[:, w0:w0 + PW]
-        for f in range(2 if n == 23 else 1):
-            m = 8 if n == 23 else 16
+        m = 8 if n >= 22 else 16
+        for f in range(16 // m):
+            if o in last:
+                vw(last[o][f])
             acc = T.acc[:, 256 * o + 128 * f:256 * o + 128 * f + 16 * m]
-            last[o] = tt(acc, win.indirect(T.lst[:, 32 * h + 8 * f:32 * h + 8 * f + m]), acc, ADD)
+            a = tt(acc, win.indirect(T.lst[:, 32 * h + 8 * f:32 * h + 8 * f + m]), acc, ADD)
+            last[o] = [a, a] if m == 16 else ([a, last[o][1]] if f == 0 else [last[o][0], a])
             if h == 7:
-                wait("y", "sv", last[o])
+                wait("y", "sv", a)
                 Y.dma_start(T.y[:, 256 * o + 128 * f:256 * o + 128 * f + 16 * m], acc).then_inc(T.sem.dy, 16)
-        gath.append(last[o])
+        gath.append(a)
 
     wait("y", "dy", 64)
     wait("y", "dn", 128)

from concourse.bass import DstId, RemoteDMATransfer
from concourse.mybir import dt, AluOpType, ActivationFunctionType

NP = 8
PW = 384
CAP = 64

SCRATCH = {}


def _bufs(dtype, names):
    for item in names.split():
        name, width = item.split(":")
        SCRATCH[name] = ("sbuf", [128, int(width)], dtype)


_bufs("bfloat16", "xb:1040 usb:32 usr:512 zt:8192 zb:1024 wf:1536 hb:512 mb:1024 n16:256 mk:256 rst:256")
_bufs("float8_e4m3fn_x4", "uq:128 xq:256 hq:128 mq:256 wfq:384 wq:3072 lc:320")
_bufs("uint8", "up:128 xp:256 hp:128 mp:256 wfp:384 wp:3072 lp:320")
_bufs("int32", "pidx:1 pci:3 oi:16 oj:16")
_bufs("uint16", "ul:32 offu:16 cl:16 ml:64 ru:64 lst:256")
_bufs("float32", "ia:32 pcf:4 n4:64 mk4:64 rst4:64 tc65:16 tc64:16 j4:256 im:16 mj:16 c96:96 rk:96")
_bufs("float32", "sm:256 sc:256 srep:16 sl:96 ga:96 eo:16 xo:32 cop:40 exo:32 bto:32 n1:16 n2:16 zz:16 wd:384 wm:64 ws:64 n3:16")
_bufs("float32", "m1:48 c1:48 m01:16 m12:16 c2:16 aa:48 ee:96 cs:96 ctp:104 ex:96 bt:96 eb:96 kk:96 ke:96 t48:48 t16:16 x32:32 xt:32 xx:64 xr:64")
_bufs("float32", "we:96 w48:48 w16:16 x33:32 wt:32 acc:768")
_bufs("float32", "pw:%d" % (NP * PW))
for _b in range(8):
    SCRATCH["ps%d" % _b] = ("psum", [128, 512], "float32")

SEMAPHORES = ["sv", "ss", "st", "sg", "dx", "du", "dwf", "rc", "ls", "dn", "dy"]
SEMAPHORES += ["dl%d" % _a for _a in range(4)] + ["dw%d" % _a for _a in range(6)] + ["rs%d" % _a for _a in range(6)]

ADD, SUB, MUL, AND = AluOpType.add, AluOpType.subtract, AluOpType.mult, AluOpType.bitwise_and
MAX, GT, GE, EQ = AluOpType.max, AluOpType.is_gt, AluOpType.is_ge, AluOpType.is_equal
COPY = ActivationFunctionType.Copy


def rank_program(g, core, T, topo):
    r = T.rank_of(core)
    if r is None:
        return
    N = len(T.cores)
    others = [s for s in range(N) if s != r]
    order = [s for s in range(N) if s % 2 == 0] + [s for s in range(N) if s % 2 == 1]

    queues = {"g": g, "v": g.vector, "s": g.scalar, "t": g.tensor, "y": g.sync}
    V, S, TE, Y = g.vector, g.scalar, g.tensor, g.sync
    count = {"sv": 0, "ss": 0, "st": 0, "sg": 0}
    seen = {}

    def wait(q, sem, n):
        if n > seen.get((q, sem), 0):
            queues[q].wait_ge(T.sem[sem], n)
            seen[(q, sem)] = n

    def done(sem, ins):
        ins.then_inc(T.sem[sem], 1)
        count[sem] += 1
        return count[sem]

    def v(ins):
        return done("sv", ins)

    def s_(ins):
        return done("ss", ins)

    def t_(ins):
        return done("st", ins)

    def vw(n):
        wait("v", "sv", n)

    def tt(out, a, b, op):
        return v(V.tensor_tensor(out, a, b, op))

    def ts(out, a, scalar, op):
        return v(V.tensor_scalar(out, a, scalar, None, op))

    def scan(out, a, b, op0, op1):
        return v(V.tensor_tensor_scan(out, a, b, 0.0, op0, op1))

    S.dma_start(T.usb[:, :], T.us[:, 0:32]).then_inc(T.sem.du, 16)
    Y.dma_start(T.xb[:, 0:1024], T.x[:, :]).then_inc(T.sem.dx, 16)

    def iota(out, pattern, base=0, cm=0, flag=True):
        if flag:
            return done("sg", g.iota(out, pattern, base, cm, allow_small_or_imprecise_dtypes=True))
        return done("sg", g.iota(out, pattern, base, cm))

    i_p = iota(T.pidx[:, :], [[1, 1]], 0, 1, False)
    i_a = iota(T.ia[:, :], [[4, 8], [0, 4]])
    i_n16 = iota(T.n16[:, :], [[0, 16], [1, 16]])
    iota(T.oi[:, :], [[1, 16]], 0, 16, False)
    iota(T.n4[:, :], [[0, 16], [1, 4]])
    iota(T.im[:, :], [[64, 16]], -1024)
    i_j4 = iota(T.j4[:, :], [[4, 256]])
    i_c0 = iota(T.c96[:, :], [[0, 96]])
    wait("g", "sg", i_c0)
    for e, s in enumerate(order):
        slot = others.index(s) if s != r else N - 1
        iota(T.c96[:, 16 * e:16 * e + 1], [[1, 1]], CAP * slot - 1)

    wait("v", "sg", i_p)
    ts(T.pci[:, 1:2], T.pidx[:, :], 3, AND)
    ts(T.pci[:, 0:1], T.pidx[:, :], 15, AND)
    a = v(V.tensor_scalar(T.pci[:, 2:3], T.pidx[:, :], 2, 3, AluOpType.logical_shift_right, AND))
    c_zb = v(V.memset(T.zb[:, :], 0.0))
    vw(a)
    a = v(V.tensor_copy(T.pcf[:, 0:3], T.pci[:, :]))
    c_z0 = v(V.memset(T.zt[:, 0:2048], 0.0))
    vw(a)
    wait("v", "sg", i_a)
    c_ul = ts(T.ul[:, :], T.ia[:, :], T.pcf[:, 1:2], ADD)
    v(V.memset(T.xb[:, 1024:1040], 0.0))
    wait("v", "du", 16)
    vw(c_ul)
    c_u = v(V.tensor_copy(T.usr[:, 0:256], T.usb[:, 0:32].indirect(T.ul[:, 0:16])))
    wait("s", "du", 16)
    wait("s", "sv", c_ul)
    s_u = s_(S.activation(T.usr[:, 256:512], T.usb[:, 0:32].indirect(T.ul[:, 16:32]), COPY))
    wait("v", "sg", i_n16)
    ts(T.rst[:, :], T.n16[:, :], 0.0, GT)
    wait("s", "sv", c_zb)
    s_z = [s_(S.activation(T.zt[:, 2048 + 1024 * k:3072 + 1024 * k], T.zb[:, :], COPY)) for k in range(6)]
    vw(c_u)
    wait("v", "ss", s_u)
    v(V.quantize_mx(T.uq[:, :], T.up[:, :], T.usr[:, :]))
    wait("v", "dx", 16)
    c_xq = v(V.quantize_mx(T.xq[:, :], T.xp[:, :], T.xb[:, 0:1024]))
    c_mk = ts(T.mk[:, :], T.n16[:, :], T.pcf[:, 0:1], EQ)

    place = [0, 2048, 4096, 6144, 0, 2048]

    def load_w(c):
        o, f = c // 2, 4 * (c % 2)
        for h in range(f, f + 4):
            z = place[c] + 512 * (h - f)
            Y.dma_start(T.zt[16 * h:16 * h + 16, z:z + 512],
                        T.w[16 * h:16 * h + 16, 512 * o:512 * o + 512]).then_inc(T.sem["dw%d" % c], 16)

    c_w = {}

    def quant_w(c):
        wait("v", "dw%d" % c, 64)
        c_w[c] = v(V.quantize_mx(T.wq[:, 512 * c:512 * c + 512], T.wp[:, 512 * c:512 * c + 512],
                                 T.zt[:, place[c]:place[c] + 2048]))

    wait("y", "dx", 16)
    wait("y", "sv", c_z0)
    load_w(0)
    wait("y", "ss", s_z[1])
    load_w(1)
    Y.dma_start(T.wf[:, :], T.w[:, :]).then_inc(T.sem.dwf, 16)
    wait("y", "ss", s_z[3])
    load_w(2)

    wait("t", "sv", c_xq)
    p_s = t_(TE.matmul_mx(T.ps0[:, 0:256], T.uq[:, 0:128], T.up[:, 0:128], T.xq[:, 0:256], T.xp[:, 0:256], True, True))
    wait("v", "st", p_s)
    vw(c_mk)
    c_ps0 = tt(T.sm[:, :], T.ps0[:, 0:256], T.mk[:, :], MUL)
    vw(c_ps0)
    a = scan(T.sc[:, :], T.rst[:, :], T.sm[:, :], MUL, ADD)
    vw(a)
    c_so = v(V.tensor_copy(T.srep[:, 0:16], T.sc[:, 15:256:16]))

    turn = [(r + k) % N for k in range(1, N)]
    dst_ids, emask = [], None
    for s in turn:
        rid, pid, _se = topo.addr(T.cores[s])
        dst_ids.append(DstId(rid=rid, pnc=pid))
        m = topo.mask(core, T.cores[s])
        emask = m if emask is None else emask & m
    ne = len([b for b in range(16) if emask >> b & 1])

    def send(src, dsts, sem):
        g.remote_dma_fused([RemoteDMATransfer(dst_ids=dst_ids, dma_engine_mask=emask, remote_sem=T.sem[sem],
                                              srcs=[src], dsts=dsts)], local_sem=T.sem.ls)

    e0 = order.index(r)
    wait("g", "sv", c_so)
    send(T.srep[:, 0:16], [T.sl[:, 16 * e0:16 * e0 + 16] for _s in turn], "rs%d" % r)

    iota(T.xo[:, 16:32], [[0, 16]])
    iota(T.cop[:, 0:1], [[0, 1]])
    i_z1 = iota(T.wd[:, 0:64], [[0, 64]])
    iota(T.ctp[:, 0:1], [[0, 1]])
    iota(T.x32[:, 16:32], [[0, 16]])
    iota(T.x33[:, 16:32], [[0, 16]])
    i_rk = iota(T.rk[:, :], [[1, 2], [2, 3], [0, 16]])

    wait("v", "sg", i_j4)
    ts(T.oj[:, :], T.oi[:, :], 255, AND)
    a = ts(T.pcf[:, 3:4], T.pcf[:, 0:1], 4.0, MUL)
    v(V.memset(T.hb[:, 256:512], 0.0))
    ts(T.mk4[:, :], T.n4[:, :], T.pcf[:, 2:3], EQ)
    ts(T.rst4[:, :], T.n4[:, :], 0.0, GT)
    vw(max(a, c_so))
    v(V.tensor_copy(T.sl[:, 16 * e0:16 * e0 + 16], T.srep[:, 0:16]))
    ts(T.tc65[:, :], T.oj[:, :], 65.0, ADD)
    ts(T.tc64[:, :], T.oj[:, :], 64.0, ADD)
    c_cst = ts(T.mj[:, :], T.im[:, :], T.pcf[:, 3:4], ADD)
    quant_w(0)
    wait("y", "sv", c_w[0])
    load_w(4)
    wait("y", "ss", s_z[5])
    load_w(3)
    quant_w(1)
    wait("y", "sv", c_w[1])
    load_w(5)

    at = {}

    def r01():
        tt(T.m1[:, :], T.sl[:, 0:48], T.sl[:, 48:96], MAX)
        return tt(T.c1[:, :], T.sl[:, 48:96], T.sl[:, 0:48], GT)

    def r02():
        tt(T.m12[:, :], T.m1[:, 16:32], T.m1[:, 32:48], MAX)
        tt(T.c2[:, :], T.m1[:, 16:32], T.m1[:, 0:16], GT)
        return tt(T.m01[:, :], T.m1[:, 0:16], T.m1[:, 16:32], MAX)

    def r03():
        tt(T.aa[:, 0:16], T.m1[:, 0:16], T.m12[:, :], GE)
        return tt(T.aa[:, 32:48], T.m1[:, 32:48], T.m01[:, :], GT)

    def r04():
        return tt(T.aa[:, 16:32], T.c2[:, :], T.aa[:, 32:48], GT)

    def r05():
        return tt(T.ee[:, 48:96], T.aa[:, :], T.c1[:, :], MUL)

    def r06():
        return tt(T.ee[:, 0:48], T.aa[:, :], T.ee[:, 48:96], SUB)

    def r07():
        a = scan(T.cs[:, :], T.rst[:, 0:96], T.ee[:, :], MUL, ADD)
        wait("v", "sg", i_rk)
        tt(T.eb[:, :], T.ee[:, :], T.c96[:, :], ADD)
        return a

    def r08():
        return v(V.transpose(T.ctp[:, 1:97], T.cs[:, :]))

    def r09():
        return scan(T.ex[:, :], T.ctp[:, 0:96], T.rst[:, 0:96], ADD, MUL)

    def r10():
        return v(V.transpose(T.bt[:, :], T.ex[:, :]))

    def r11():
        return tt(T.eb[:, 0:96:16], T.eb[:, 0:96:16], T.bt[:, 15:96:16], ADD)

    def r12():
        return scan(T.kk[:, :], T.rst[:, 0:96], T.eb[:, :], MUL, ADD)

    def r13():
        return tt(T.ke[:, :], T.kk[:, :], T.ee[:, :], MUL)

    def r14():
        return tt(T.t48[:, :], T.ke[:, 0:48], T.ke[:, 48:96], ADD)

    def r15():
        return tt(T.t16[:, :], T.t48[:, 0:16], T.t48[:, 16:32], ADD)

    def r16():
        return tt(T.x32[:, 0:16], T.t16[:, :], T.t48[:, 32:48], ADD)

    def r17():
        return v(V.transpose(T.xt[:, :], T.x32[:, :]))

    def r18():
        for d in range(2):
            for h in range(2):
                a = v(V.tensor_copy(T.xx[:, 32 * d + 16 * h:32 * d + 16 * h + 16], T.xt[:, 16 * d:16 * d + 16]))
        return a

    def r19():
        return v(V.transpose(T.xr[:, :], T.xx[:, :]))

    def r20():
        return v(V.tensor_copy(T.ru[:, :], T.xr[:, :]))

    steps = [r01, r02, r03, r04, r05, r06, r07, r08, r09, r10, r11, r12, r13, r14, r15, r16, r17, r18, r19, r20]
    own = []

    def fill():
        k = len(at)
        if k < len(steps):
            if k:
                vw(at[k - 1])
            at[k] = steps[k]()

    def after(n):
        own.append(n)
        if len(own) % 2 == 1 or len(own) > 11:
            fill()
        vw(n)

    wait("v", "sg", i_z1)
    vw(c_cst)
    c_eo = None
    for s in reversed(turn):
        wait("v", "rs%d" % s, ne)
        e = order.index(s)
        op = GT if s < r else GE
        if c_eo is None:
            c_eo = tt(T.eo[:, :], T.srep[:, 0:16], T.sl[:, 16 * e:16 * e + 16], op)
        else:
            k = 16 * turn.index(s)
            a = tt(T.ga[:, k:k + 16], T.srep[:, 0:16], T.sl[:, 16 * e:16 * e + 16], op)
            vw(a)
            c_eo = tt(T.eo[:, :], T.eo[:, :], T.ga[:, k:k + 16], MUL)
    after(c_eo)
    c_co = scan(T.xo[:, 0:16], T.rst[:, 0:16], T.eo[:, :], MUL, ADD)
    c_n1 = tt(T.n1[:, :], T.eo[:, :], T.tc65[:, :], MUL)
    after(c_co)
    a = v(V.transpose(T.cop[:, 1:33], T.xo[:, :]))
    vw(c_n1)
    c_n2 = tt(T.n2[:, :], T.tc64[:, :], T.n1[:, :], SUB)
    after(a)
    a = scan(T.exo[:, :], T.cop[:, 0:32], T.rst[:, 0:32], ADD, MUL)
    vw(c_n2)
    tt(T.zz[:, :], T.xo[:, 0:16], T.n2[:, :], ADD)
    after(a)
    a = v(V.transpose(T.bto[:, :], T.exo[:, :]))
    after(a)
    a = ts(T.offu[:, :], T.zz[:, :], T.bto[:, 15:16], ADD)
    after(a)
    a = v(V.tensor_copy(T.wd[:, 0:384].indirect(T.offu[:, 0:16]), T.j4[:, :]))
    after(a)
    a = tt(T.wm[:, :], T.wd[:, 0:64], T.mk4[:, :], MUL)
    after(a)
    a = scan(T.ws[:, :], T.rst4[:, :], T.wm[:, :], MUL, ADD)
    after(a)
    c_cl = ts(T.cl[:, :], T.ws[:, 3:64:4], T.pcf[:, 1:2], ADD)
    wait("s", "sv", c_cl)
    wait("s", "dx", 16)
    s_h = s_(S.activation(T.hb[:, 128:256], T.xb[:, 0:1040].indirect(T.cl[:, 8:16]), COPY))
    after(c_cl)
    a = v(V.tensor_copy(T.hb[:, 0:128], T.xb[:, 0:1040].indirect(T.cl[:, 0:8])))
    c_n3 = tt(T.n3[:, :], T.eo[:, :], T.mj[:, :], MUL)
    after(a)
    wait("v", "ss", s_h)
    c_hq = v(V.quantize_mx(T.hq[:, :], T.hp[:, :], T.hb[:, :]))
    wait("g", "sv", c_hq)
    lands = []
    for s in turn:
        k = [q for q in range(N) if q != s].index(r)
        lands.append((CAP * k, CAP * k + CAP))
    send(T.hq[:, 0:CAP].bitcast(dt.uint8), [T.lc[:, b:e].bitcast(dt.uint8) for b, e in lands], "rc")
    send(T.hp[:, 0:CAP], [T.lp[:, b:e] for b, e in lands], "rc")
    for k in range(NP):
        i_p0 = iota(T.pw[:, PW * k + 320:PW * k + PW], [[0, 64]])

    vw(c_n3)
    for t in range(4):
        c_ml = ts(T.ml[:, 16 * t:16 * t + 16], T.n3[:, :], 1024.0 + t, ADD)
    wait("s", "sv", c_ml)
    for t in range(4):
        s_m = s_(S.activation(T.mb[:, t:1024:4], T.xb[:, 0:1040].indirect(T.ml[:, 16 * t:16 * t + 16]), COPY))
    while len(at) < 7:
        fill()
    vw(at[5])
    a = tt(T.we[:, :], T.ee[:, :], T.rk[:, :], MUL)
    after(a)
    a = tt(T.w48[:, :], T.we[:, 0:48], T.we[:, 48:96], ADD)
    after(a)
    a = tt(T.w16[:, :], T.w48[:, 0:16], T.w48[:, 16:32], ADD)
    after(a)
    a = tt(T.x33[:, 0:16], T.w16[:, :], T.w48[:, 32:48], ADD)
    after(a)
    c_wt = v(V.transpose(T.wt[:, :], T.x33[:, :]))
    while len(at) < len(steps):
        fill()
    c_ru = at[len(steps) - 1]
    for k in range(4):
        for b in range(4):
            q = "y" if b % 2 == 0 else "s"
            wait(q, "sv", c_ru)
            queues[q].dma_start(T.lst[32 * b:32 * b + 32, 64 * k:64 * k + 64],
                                T.ru[32 * k:32 * k + 32, :]).then_inc(T.sem["dl%d" % k], 16)
    wait("y", "sv", c_wt)
    for k in range(4):
        for h in range(2):
            Y.dma_start(T.wn[2 * k + h:2 * k + h + 1, :],
                        T.wt[32 * k:32 * k + 16, 16 * h:16 * h + 16]).then_inc(T.sem.dn, 16)

    wait("v", "dwf", 16)
    v(V.quantize_mx(T.wfq[:, :], T.wfp[:, :], T.wf[:, :]))
    wait("v", "ss", s_m)
    c_mq = v(V.quantize_mx(T.mq[:, :], T.mp[:, :], T.mb[:, :]))
    wait("t", "sv", c_mq)
    bank_free = [("sv", c_ps0)] + [None] * 7
    p_m = [t_(TE.matmul_mx(T["ps%d" % (1 + o)][:, 0:256], T.wfq[:, 128 * o:128 * o + 128],
                           T.wfp[:, 128 * o:128 * o + 128], T.mq[:, 0:256], T.mp[:, 0:256], True, True)) for o in range(3)]
    for o in range(3):
        wait("s", "st", p_m[o])
        bank_free[1 + o] = ("ss", s_(S.activation(T.acc[:, 256 * o:256 * o + 256], T["ps%d" % (1 + o)][:, 0:256], COPY)))
    for c in range(2, 6):
        quant_w(c)

    wait("t", "rc", 2 * ne * len(others))
    wait("v", "sg", i_p0)
    items = [(o, h) for h in range(5) for o in (0, 1)]
    items += [(0, 5), (2, 0), (0, 6), (2, 1), (0, 7), (2, 2), (1, 5), (2, 3), (1, 6), (2, 4), (1, 7), (2, 5), (2, 6), (2, 7)]
    gath, last = [], {}
    for n, (o, h) in enumerate(items):
        bank = T["ps%d" % (n % 8)]
        wait("t", "sv", c_w[2 * o + h // 4])
        if bank_free[n % 8] is not None:
            wait("t", *bank_free[n % 8])
        w = 1024 * o + 128 * h
        p = t_(TE.matmul_mx(bank[:, 0:320], T.wq[:, w:w + 128], T.wp[:, w:w + 128], T.lc[:, 0:320], T.lp[:, 0:320], True, True))
        w0 = PW * (n % NP)
        if n >= NP:
            wait("s", "sv", gath[n - NP])
        wait("s", "st", p)
        c = s_(S.activation(T.pw[:, w0:w0 + 320], bank[:, 0:320], COPY))
        bank_free[n % 8] = ("ss", c)
        wait("v", "ss", c)
        wait("v", "dl%d" % (h // 2), 64)
        win = T.pw[:, w0:w0 + PW]
        m = 8 if n >= 22 else 16
        for f in range(16 // m):
            if o in last:
                vw(last[o][f])
            acc = T.acc[:, 256 * o + 128 * f:256 * o + 128 * f + 16 * m]
            a = tt(acc, win.indirect(T.lst[:, 32 * h + 8 * f:32 * h + 8 * f + m]), acc, ADD)
            last[o] = [a, a] if m == 16 else ([a, last[o][1]] if f == 0 else [last[o][0], a])
            if h == 7:
                wait("y", "sv", a)
                Y.dma_start(T.y[:, 256 * o + 128 * f:256 * o + 128 * f + 16 * m], acc).then_inc(T.sem.dy, 16)
        gath.append(a)

    wait("y", "dy", 64)
    wait("y", "dn", 128)
    wait("g", "ls", 3 * ne)
    for sem in ("sv", "ss", "st", "sg"):
        wait("g", sem, count[sem])
